import numpy as np, ml_dtypes
CORES = [10,34,74,98]
N = 4
import mx_ref
BF = ml_dtypes.bfloat16
def cols(t, e):
    v = np.concatenate([t.reshape(128, -1, 4), np.zeros((128, 1, 4), BF)], axis=1)
    return np.ascontiguousarray(v[:, e]).reshape(128, -1)
def tile(rs):
    return np.stack(rs, axis=2).reshape(128, -1).astype(BF)
def cut(t, i, w=512):
    return t[:, w * i:w * i + w]
def f(rng, *shape):
    return mx_ref.flush((rng.standard_normal(shape, dtype=np.float32) * np.exp2(rng.integers(-2, 3, shape[:-1] + (1,)))).astype(BF))
def wide(rng, *shape, cols=0):
    v = rng.standard_normal(shape, dtype=np.float32) * np.exp2(rng.integers(-12, 13, shape)).astype(np.float32)
    if cols: v *= np.repeat(np.exp2(rng.integers(-cols, cols + 1, shape[:-2] + (1, shape[-1] // 4))) * (rng.random(shape[:-2] + (1, shape[-1] // 4)) > 0.0625), 4, axis=-1).astype(np.float32)
    return mx_ref.flush(v.astype(BF))
T, ST = 512, 128
def flags(rng, n, new):
    s = np.zeros((N, T), bool)
    for r in range(N):
        s[r, 0] = new[r] > 0
        s[r, 1 + rng.permutation(T - 1)[:int(n[r]) - int(new[r])]] = True
    return s
def borders(rng):
    new = rng.integers(0, 2, N); new[0] = 1
    return new
def make(rng, s, far=2, spread=False):
    t = np.zeros((128, 128, 4), np.float32); t[:, :16] = rng.standard_normal((128, 16, 4), dtype=np.float32)
    if spread: t[64:] = 0
    t = mx_ref.flush(t.reshape(128, 512).astype(BF))
    k = (rng.integers(0, 16) + np.cumsum(s.reshape(-1) * rng.integers(1, 16, N * T))) % 16
    c = t.astype(np.float32).reshape(128, 128, 4)[:, k] + rng.standard_normal((128, N * T, 4), dtype=np.float32) * np.float32(0.125)
    if spread: c[64:] = wide(rng, 64, 4 * N * T).astype(np.float32).reshape(64, N * T, 4)
    c = c * np.exp2(rng.integers(-far, far + 1, (N * T, 1))).astype(np.float32)
    x = np.ascontiguousarray(c.reshape(128, N, 4 * T).transpose(1, 0, 2)).astype(BF)
    return {"x": mx_ref.flush(x), "p": np.stack([t] * N), "a": f(rng, N, 128, 2048), "w": f(rng, N, 128, 512), "v": f(rng, N, 128, 512)}
def setup_inputs(rng):
    return make(rng, flags(rng, rng.integers(1, ST + 1, N), borders(rng)))
def setup_inputs_border(rng):
    return make(rng, flags(rng, rng.integers(1, ST + 1, N), np.arange(N) == 0))
def setup_inputs_dense(rng):
    n = np.full(N, ST); n[0] = ST - rng.integers(1, N)
    return make(rng, flags(rng, n, borders(rng)))
def setup_inputs_one(rng):
    return make(rng, flags(rng, np.ones(N, int), np.arange(N) == 0))
def setup_inputs_spread(rng):
    return make(rng, flags(rng, rng.integers(1, ST + 1, N), borders(rng)), far=8, spread=True)
def setup_inputs_ties(rng):
    d = setup_inputs(rng)
    m = np.cumsum(flags(rng, rng.integers(1, ST + 1, N), borders(rng)).reshape(-1)) - 1; n = int(m[-1]) + 1
    u = np.zeros((128, 8, 4), np.float32); u[:64] = rng.choice([-1, 1], (64, 8, 4)) * rng.uniform(0.75, 1.25, (64, 8, 4))
    g = np.zeros((128, 1, 4), np.float32); g[64:] = rng.choice([-1, 1], (64, 1, 4))
    t = np.zeros((128, 128, 4), np.float32); t[:, :8] = u + g; t[:, 8:16] = u + g
    k = np.cumsum(rng.integers(1, 8, n)) % 8
    big = int(np.argmax(np.bincount(m)))
    k = (k - k[big]) % 8
    neg = rng.permutation(n) % 2
    c = u[:, k[m]] + g * np.where(neg[m] > 0, -2, 1).astype(np.float32)[:, None] + rng.standard_normal((128, N * T, 4), dtype=np.float32) * np.float32(0.125)
    c = c * np.exp2(rng.integers(-2, 3, (N * T, 1))).astype(np.float32)
    zero = (k[m] == 0) & (rng.random(N * T) < 0.25); zero[np.flatnonzero(m == big)[1]] = True
    c[:, zero] = 0
    d["x"] = mx_ref.flush(np.ascontiguousarray(c.reshape(128, N, 4 * T).transpose(1, 0, 2)).astype(BF))
    d["p"] = np.stack([mx_ref.flush(t.reshape(128, 512).astype(BF))] * N)
    return d
def labels(x, p):
    return np.stack([np.argmax(mx_ref.matmul(mx_ref.quantize(p[r]), mx_ref.quantize(x[r]))[:16] + np.float32(0.0), axis=0) for r in range(N)])
def starts(l):
    e = l.reshape(-1)
    return np.concatenate([[True], e[1:] != e[:-1]])
def check_inputs(d):
    b = []
    for r in range(N):
        if not np.array_equal(d["p"][r], d["p"][0]): b.append("p (the same on all ranks)")
        if d["p"][r][:, 64:].astype(np.float32).any(): b.append("p (zero columns)")
    n = starts(labels(d["x"], d["p"])).reshape(N, T).sum(axis=1)
    if n.min() < 1 or n.max() > ST: b.append("x (runs that start on a rank)")
    return b
def reference(x, p, a, w, v):
    l = labels(x, p); s = starts(l)
    m = np.add.accumulate(s.astype(int)) - 1
    first = np.flatnonzero(s)
    seq = np.concatenate([x[r] for r in range(N)], axis=1)
    h = []
    for r in range(N):
        e = np.full(ST, -1); mine = first[r::N]; e[:len(mine)] = mine
        c = mx_ref.quantize(cols(seq, e))
        h.append(tile([np.maximum(mx_ref.matmul(mx_ref.quantize(np.ascontiguousarray(cut(a[r], i))), c), np.float32(0)) * np.float32(0.05) for i in range(4)]))
    h = np.concatenate(h, axis=1)
    y = np.zeros((N, 128, T), np.float32); lb = np.zeros((N, 2, T), np.float32)
    for r in range(N):
        k = m[r * T:r * T + T]
        hk = mx_ref.quantize(cols(h, (k % N) * ST + k // N))
        y[r] = mx_ref.matmul(mx_ref.quantize(w[r]), mx_ref.quantize(x[r])) + mx_ref.matmul(mx_ref.quantize(v[r]), hk)
        lb[r, 0] = l[r]; lb[r, 1] = k
    return {"y": y, "lb": lb}

@@ -1,0 +1,451 @@
+from concourse.bass import DstId, RemoteDMATransfer
+from concourse.mybir import dt, AluOpType, AxisListType, ActivationFunctionType
+
+ALU = AluOpType
+ACT = ActivationFunctionType
+N = 4
+G = 34
+GT = 4 * G
+GB = G + 2
+LAND = 144
+OWN = LAND - GT
+BIG = 1e25
+DUMP = 192
+
+SCRATCH = {
+    "pb": ("sbuf", [128, 64], "bfloat16"),
+    "pt": ("sbuf", [128, 576], "bfloat16"),
+    "xb": ("sbuf", [128, 2064], "bfloat16"),
+    "ab": ("sbuf", [128, 2048], "bfloat16"),
+    "wb": ("sbuf", [128, 512], "bfloat16"),
+    "vb": ("sbuf", [128, 512], "bfloat16"),
+    "pq": ("sbuf", [128, 144], "float8_e4m3fn_x4"), "pz": ("sbuf", [128, 144], "uint8"),
+    "xq": ("sbuf", [128, 512], "float8_e4m3fn_x4"), "xz": ("sbuf", [128, 512], "uint8"),
+    "aq": ("sbuf", [128, 512], "float8_e4m3fn_x4"), "az": ("sbuf", [128, 512], "uint8"),
+    "wq": ("sbuf", [128, 128], "float8_e4m3fn_x4"), "wz": ("sbuf", [128, 128], "uint8"),
+    "vq": ("sbuf", [128, 128], "float8_e4m3fn_x4"), "vz": ("sbuf", [128, 128], "uint8"),
+    "cq": ("sbuf", [128, 256], "float8_e4m3fn_x4"), "cz": ("sbuf", [128, 256], "uint8"),
+    "hq": ("sbuf", [128, 256], "float8_e4m3fn_x4"), "hz": ("sbuf", [128, 256], "uint8"),
+    "sc": ("sbuf", [128, 256], "float32"),
+    "rs": ("sbuf", [128, 136], "float32"),
+    "xm": ("sbuf", [128, 264], "float32"),
+    "nn": ("sbuf", [128, 256], "bfloat16"),
+    "cc": ("sbuf", [128, 256], "bfloat16"),
+    "la": ("sbuf", [128, 32], "bfloat16"),
+    "lr": ("sbuf", [128, 32], "bfloat16"),
+    "eq": ("sbuf", [128, 32], "float32"),
+    "one": ("sbuf", [128, 32], "float32"),
+    "zb": ("sbuf", [128, 32], "bfloat16"),
+    "cnt": ("sbuf", [128, 32], "float32"),
+    "ncx": ("sbuf", [128, 32], "float32"),
+    "ex": ("sbuf", [128, 96], "bfloat16"),
+    "rw": ("sbuf", [128, 96], "bfloat16"),
+    "pr": ("sbuf", [128, 32], "float32"),
+    "pm": ("sbuf", [128, 32], "float32"),
+    "col": ("sbuf", [128, 16], "float32"),
+    "msg": ("sbuf", [128, 2], "uint16"),
+    "msgin": ("sbuf", [128, 4], "uint16"),
+    "pi": ("sbuf", [128, 8], "int32"),
+    "pf": ("sbuf", [128, 8], "float32"),
+    "row": ("sbuf", [128, 16], "float32"),
+    "mk": ("sbuf", [128, 32], "float32"),
+    "kd": ("sbuf", [128, 32], "float32"),
+    "mu": ("sbuf", [128, GT], "float32"),
+    "rt": ("sbuf", [128, GT], "float32"),
+    "rt2": ("sbuf", [128, GT // 2], "float32"),
+    "cf": ("sbuf", [128, G], "float32"),
+    "jv": ("sbuf", [128, 512], "float32"),
+    "u": ("sbuf", [128, 32], "float32"),
+    "nk": ("sbuf", [128, 32], "float32"),
+    "of": ("sbuf", [128, 32], "float32"),
+    "of16": ("sbuf", [128, 32], "uint16"),
+    "fw": ("sbuf", [128, DUMP + 512], "float32"),
+    "fm": ("sbuf", [128, 128], "float32"),
+    "f2": ("sbuf", [128, 64], "float32"),
+    "f4": ("sbuf", [128, 32], "float32"),
+    "ls16": ("sbuf", [128, 32], "uint16"),
+    "xg": ("sbuf", [128, 560], "bfloat16"),
+    "sh16": ("sbuf", [128, G], "uint16"),
+    "sx": ("sbuf", [128, 4 * GT], "bfloat16"),
+    "vi": ("sbuf", [128, 4], "int32"),
+    "fi": ("sbuf", [128, 4], "int32"),
+    "li": ("sbuf", [128, 4], "int32"),
+    "ni": ("sbuf", [128, 4], "int32"),
+    "qi": ("sbuf", [128, 4], "int32"),
+    "df": ("sbuf", [128, 4], "float32"),
+    "ei": ("sbuf", [128, 4], "int32"),
+    "hb": ("sbuf", [128, 4 * GT], "bfloat16"),
+    "t1": ("sbuf", [128, 16], "bfloat16"),
+    "t2": ("sbuf", [128, 16], "bfloat16"),
+    "in2": ("sbuf", [128, 32], "bfloat16"),
+    "ut": ("sbuf", [128, 32], "bfloat16"),
+    "wi": ("sbuf", [128, 32], "int32"),
+    "zi": ("sbuf", [128, 32], "int32"),
+    "bi": ("sbuf", [128, 32], "int32"),
+    "ki": ("sbuf", [128, 32], "int32"),
+    "gf": ("sbuf", [128, 32], "float32"),
+    "cm": ("sbuf", [128, 32], "float32"),
+    "gx": ("sbuf", [128, 32], "float32"),
+    "bf": ("sbuf", [128, 32], "float32"),
+    "ix": ("sbuf", [128, 32], "float32"),
+    "ix16": ("sbuf", [128, 32], "uint16"),
+    "hv": ("sbuf", [128, 4 * GB], "float32"),
+    "wx": ("sbuf", [128, 512], "float32"),
+    "yb": ("sbuf", [128, 512], "float32"),
+    "lb0": ("sbuf", [128, 32], "float32"),
+    "lb1": ("sbuf", [128, 32], "float32"),
+    "pl0": ("psum", [128, 512], "float32"),
+    "pl1": ("psum", [128, 512], "float32"),
+    "pwx": ("psum", [128, 512], "float32"),
+    "pa0": ("psum", [128, 512], "float32"),
+    "pa1": ("psum", [128, 512], "float32"),
+    "pa2": ("psum", [128, 512], "float32"),
+    "pa3": ("psum", [128, 512], "float32"),
+    "pv": ("psum", [128, 512], "float32"),
+}
+DMAS = ["dp", "dx0", "dx1", "dx2", "dx3", "da", "dw", "dv", "dl0", "dl1", "dy0", "dy1"]
+SEMAPHORES = ["sv", "sa", "st", "sg", "mrecv", "mloc", "crecv", "cloc", "hrecv", "hloc"] + DMAS
+
+
+def tracker(g, T):
+    queues = {"v": g.vector, "a": g.scalar, "t": g.tensor, "g": g, "s": g.sync}
+    know = {q: {} for q in queues}
+    count = {}
+    acc = {}
+    order = [0]
+
+    def wait(q, tok):
+        sem, n, snap = tok
+        if know[q].get(sem, 0) < n:
+            queues[q].wait_ge(T.sem[sem], n)
+            for k, v in snap.items():
+                if know[q].get(k, 0) < v:
+                    know[q][k] = v
+            know[q][sem] = max(n, know[q].get(sem, 0))
+
+    def settle(q, reads, writes):
+        deps = []
+        for buf, a, b in reads:
+            deps += [(o, tok) for (c, d, w, tok, o) in acc.get(buf, []) if w and a < d and c < b]
+        for buf, a, b in writes:
+            deps += [(o, tok) for (c, d, w, tok, o) in acc.get(buf, []) if a < d and c < b]
+        for o, tok in sorted(deps, key=lambda z: -z[0]):
+            wait(q, tok)
+
+    def note(tok, reads, writes):
+        order[0] += 1
+        for buf, a, b in reads:
+            acc.setdefault(buf, []).append((a, b, False, tok, order[0]))
+        for buf, a, b in writes:
+            acc.setdefault(buf, []).append((a, b, True, tok, order[0]))
+
+    def emit(q, call, reads, writes, sem=None, inc=1, chain=False):
+        settle(q, reads, [] if chain else writes)
+        sem = sem or "s" + q
+        call().then_inc(T.sem[sem], inc)
+        count[sem] = count.get(sem, 0) + inc
+        note((sem, count[sem], dict(know[q])), reads, writes)
+
+    def remote(call, reads, sem, n):
+        settle("g", reads, [])
+        call()
+        count[sem] = count.get(sem, 0) + n
+
+    def arrives(sem, n, writes):
+        count[sem] = count.get(sem, 0) + n
+        note((sem, n, {}), [], writes)
+
+    def finish():
+        for sem, n in count.items():
+            wait("g", (sem, n, {}))
+
+    return emit, remote, arrives, finish
+
+
+def rank_program(g, core, T, topo):
+    s = T.rank_of(core)
+    if s is None:
+        return
+    emit, remote, arrives, finish = tracker(g, T)
+
+    def A(name, a, b):
+        return T[name][:, a:b]
+
+    def ap(t):
+        return T[t[0]][:, t[1]:t[2]:t[3]] if len(t) > 3 else T[t[0]][:, t[1]:t[2]]
+
+    def span(t):
+        return (t[0], t[1], t[2])
+
+    def dma(q, sem, out, in_, reads, writes):
+        eng = g.sync if q == "s" else g.scalar
+        emit(q, lambda: eng.dma_start(out, in_), reads, writes, sem=sem, inc=16)
+
+    def tt(o, x, y, op):
+        emit("v", lambda: g.vector.tensor_tensor(ap(o), ap(x), ap(y), op), [span(x), span(y)], [span(o)])
+
+    def ts(o, x, s1, s2, op0, op1=None):
+        r = [span(x)] + [span(z) for z in (s1, s2) if isinstance(z, tuple)]
+        c1 = ap(s1) if isinstance(s1, tuple) else s1
+        c2 = ap(s2) if isinstance(s2, tuple) else s2
+        if op1 is None:
+            emit("v", lambda: g.vector.tensor_scalar(ap(o), ap(x), c1, None, op0), r, [span(o)])
+        else:
+            emit("v", lambda: g.vector.tensor_scalar(ap(o), ap(x), c1, c2, op0, op1), r, [span(o)])
+
+    def cp(o, x, q="v"):
+        if q == "v":
+            emit("v", lambda: g.vector.tensor_copy(ap(o), ap(x)), [span(x)], [span(o)])
+        else:
+            emit("a", lambda: g.scalar.activation(ap(o), ap(x), ACT.Copy), [span(x)], [span(o)])
+
+    def fill(o, c):
+        emit("v", lambda: g.vector.memset(ap(o), c), [], [span(o)])
+
+    def tr(o, x):
+        emit("v", lambda: g.vector.transpose(ap(o), ap(x)), [span(x)], [span(o)])
+
+    def scan(o, d0, d1, init, op0, op1):
+        emit("v", lambda: g.vector.tensor_tensor_scan(ap(o), ap(d0), ap(d1), init, op0, op1), [span(d0), span(d1)], [span(o)])
+
+    def red(o, x, op):
+        emit("v", lambda: g.vector.tensor_reduce(ap(o), ap(x), AxisListType.X, op), [span(x)], [span(o)])
+
+    def quant(cq, cz, a, src, b, n):
+        emit("v", lambda: g.vector.quantize_mx(A(cq, a, a + n), A(cz, a, a + n), A(src, 4 * b, 4 * b + 4 * n)),
+             [(src, 4 * b, 4 * b + 4 * n)], [(cq, a, a + n), (cz, a, a + n)])
+
+    def mm(o, lq, lz, a, rq, rz, b, n, start=True, stop=True):
+        emit("t", lambda: g.tensor.matmul_mx(A(o, 0, n), A(lq, a, a + 128), A(lz, a, a + 128), A(rq, b, b + n), A(rz, b, b + n), start, stop),
+             [(lq, a, a + 128), (lz, a, a + 128), (rq, b, b + n), (rz, b, b + n)], [(o, 0, 512)], chain=not start)
+
+    def iota(o, pattern, base, cm):
+        if o[0] == "pi":
+            emit("g", lambda: g.iota(ap(o), pattern, base, cm), [], [span(o)])
+        else:
+            emit("g", lambda: g.iota(ap(o), pattern, base, cm, allow_small_or_imprecise_dtypes=True), [], [span(o)])
+
+    def pick(q, o, win, width, off, a, b):
+        w = T[win][:, 0:width].indirect(T[off][:, a:b])
+        r = [(win, 0, width), (off, a, b)]
+        if q == "v":
+            emit("v", lambda: g.vector.tensor_copy(ap(o), w), r, [span(o)])
+        else:
+            emit("a", lambda: g.scalar.activation(ap(o), w, ACT.Copy), r, [span(o)])
+
+    dma("a", "dp", A("pb", 0, 64), T.p[:, 0:64], [], [("pb", 0, 64)])
+    for k in range(4):
+        dma("s" if k % 2 == 0 else "a", "dx%d" % k, A("xb", 512 * k, 512 * k + 512), T.x[:, 512 * k:512 * k + 512], [], [("xb", 512 * k, 512 * k + 512)])
+    dma("s", "da", A("ab", 0, 2048), T.a[:, 0:2048], [], [("ab", 0, 2048)])
+
+    iota(("pi", 0, 1), [[0, 1]], 0, 1)
+    iota(("row", 0, 16), [[1, 16]], 0, 0)
+    iota(("kd", 0, 32), [[16, 32]], DUMP, 0)
+    iota(("mu", 0, GT), [[0, G], [1, 4]], 0, 0)
+    for k in range(4):
+        iota(("rt", G * k, G * k + G), [[-4, G]], 4 * (G - 1) + (3 - (s + 1 + k) % N) + 1, 0)
+    iota(("jv", 0, 512), [[4, 32], [128, 16]], 0, 0)
+    fill(("pt", 0, 576), 0.0)
+    fill(("rs", 0, 136), BIG)
+    fill(("xm", 0, 1), -BIG)
+    fill(("rs", 0, 136, 16), -BIG)
+    fill(("eq", 0, 1), 0.0)
+    fill(("one", 0, 32), 1.0)
+    fill(("zb", 0, 32), 0.0)
+    fill(("pr", 16, 17), 0.0)
+    fill(("xb", 2048, 2064), 0.0)
+    fill(("xg", 0, 16), 0.0)
+    fill(("xg", 528, 560), 0.0)
+    fill(("fw", 0, 128), 2048.0)
+    ts(("pi", 1, 2), ("pi", 0, 1), 15, None, ALU.bitwise_and)
+    ts(("pi", 2, 3), ("pi", 0, 1), 3, None, ALU.bitwise_and)
+    ts(("pi", 3, 4), ("pi", 0, 1), 2, 3, ALU.logical_shift_right, ALU.bitwise_and)
+    ts(("pi", 4, 5), ("pi", 0, 1), 4, 1, ALU.logical_shift_right, ALU.bitwise_and)
+    cp(("pf", 1, 5), ("pi", 1, 5))
+    ts(("pf", 5, 6), ("pf", 2, 3), 0.25, None, ALU.mult)
+    ts(("pf", 6, 7), ("pf", 4, 5), -1.0, 1.0, ALU.mult, ALU.add)
+    ts(("mk", 0, 16), ("row", 0, 16), ("pf", 1, 2), None, ALU.is_equal)
+    ts(("mk", 16, 32), ("row", 0, 16), ("pf", 1, 2), None, ALU.is_equal)
+    ts(("kd", 0, 32), ("kd", 0, 32), ("pf", 1, 2), None, ALU.add)
+    ts(("mu", 0, GT), ("mu", 0, GT), ("pf", 3, 4), None, ALU.is_equal)
+    tt(("rt", 0, GT), ("rt", 0, GT), ("mu", 0, GT), ALU.mult)
+    tt(("rt2", 0, GT // 2), ("rt", 0, GT, 2), ("rt", 1, GT, 2), ALU.add)
+    tt(("cf", 0, G), ("rt2", 0, GT // 2, 2), ("rt2", 1, GT // 2, 2), ALU.add)
+    ts(("cf", 0, G), ("cf", 0, G), ("pf", 5, 6), None, ALU.add)
+    for k in range(4):
+        cp(("pt", 64 + 128 * k, 128 + 128 * k), ("pb", 0, 64))
+    quant("pq", "pz", 0, "pt", 0, 144)
+
+    for P in range(2):
+        pl = "pl%d" % P
+        for h in range(2):
+            c = 256 * P + 128 * h
+            quant("xq", "xz", c, "xb", c, 128)
+            mm(pl, "pq", "pz", 16 - 16 * h, "xq", "xz", c, 128, h == 0, h == 1)
+        o = 128 * P
+        tr(("sc", o, o + 128), (pl, 0, 128))
+        scan(("xm", o + 1, o + 129), ("sc", o, o + 128), ("rs", 1, 129), -BIG, ALU.max, ALU.min)
+        tt(("nn", o, o + 128), ("sc", o, o + 128), ("xm", o, o + 128), ALU.is_le)
+        scan(("cc", o, o + 128), ("nn", o, o + 128), ("nn", o, o + 128), 0.0, ALU.mult, ALU.add)
+        for h in range(2):
+            for d in range(2):
+                b = 16 * d + 8 * P + 4 * h
+                cp(("la", b, b + 4), ("cc", o + 16 * h + 15, o + 128, 32), "v" if P == 1 and h == 0 else "a")
+    tr(("lr", 0, 32), ("la", 0, 32))
+
+    for k, c in ((1, 0), (2, 31)):
+        emit("a", lambda: g.scalar.activation(A("ex", 32 * k, 32 * k + 32), A("zb", 0, 32), ACT.Identity, bias=A("lr", c, c + 1)),
+             [("zb", 0, 32), ("lr", c, c + 1)], [("ex", 32 * k, 32 * k + 32)])
+    tt(("eq", 1, 32), ("lr", 1, 32), ("lr", 0, 31), ALU.is_equal)
+    scan(("cnt", 0, 32), ("one", 0, 32), ("eq", 0, 32), 0.0, ALU.add, ALU.subtract)
+    ts(("ex", 0, 32), ("zb", 0, 32), ("cnt", 31, 32), None, ALU.add)
+    tr(("rw", 0, 96), ("ex", 0, 96))
+    tt(("pr", 17, 32), ("rw", 33, 48), ("rw", 64, 79), ALU.is_equal)
+    ts(("col", 0, 1), ("rw", 79, 80), 16.0, ("rw", 32, 33), ALU.mult, ALU.add)
+    scan(("pr", 0, 16), ("rw", 0, 16), ("pr", 16, 32), 0.0, ALU.add, ALU.subtract)
+    nn = ("pr", 15, 16)
+    later = [T.cores[d] for d in range(s + 1, N)]
+
+    def shared(src, dsts):
+        return [e for e in topo.engines(src, dsts[0]) if all(e in topo.engines(src, d) for d in dsts)]
+
+    if later:
+        ts(("msg", 0, 1), nn, 256.0, ("col", 0, 1), ALU.mult, ALU.add)
+        ids = []
+        for d in later:
+            rid, pid, _ = topo.addr(d)
+            ids.append(DstId(rid=rid, pnc=pid))
+        eng = shared(core, later)
+        remote(lambda: g.remote_dma_fused([RemoteDMATransfer(dst_ids=ids, dma_engine_mask=sum(1 << e for e in eng), remote_sem=T.sem.mrecv,
+                                                             srcs=[A("msg", 0, 1)], dsts=[A("msgin", s, s + 1) for _ in later])],
+                                          local_sem=T.sem.mloc), [("msg", 0, 1)], "mloc", len(eng))
+    if s:
+        arrives("mrecv", sum(len(shared(T.cores[r], [T.cores[d] for d in range(r + 1, N)])) for r in range(s)), [("msgin", 0, s)])
+    dma("s", "dw", A("wb", 0, 512), T.w[:, 0:512], [("pr", 0, 16)], [("wb", 0, 512)])
+    dma("s", "dv", A("vb", 0, 512), T.v[:, 0:512], [], [("vb", 0, 512)])
+    tt(("pm", 0, 32), ("pr", 0, 32), ("mk", 0, 32), ALU.mult)
+    ts(("ncx", 0, 32), ("cnt", 0, 32), -1.0, ("cnt", 31, 32), ALU.mult, ALU.add)
+    red(("eq", 0, 1), ("pm", 16, 32), ALU.add)
+    red(("col", 2, 3), ("pm", 0, 16), ALU.add)
+    ts(("col", 1, 2), nn, -1.0, None, ALU.add)
+    tt(("nk", 0, 32), ("eq", 0, 32), ("kd", 0, 32), ALU.mult)
+    ts(("u", 0, 32), ("ncx", 0, 32), nn, ("col", 2, 3), ALU.add, ALU.subtract)
+
+    tt(("of", 0, 32), ("u", 0, 32), ("nk", 0, 32), ALU.max)
+    cp(("of16", 0, 32), ("of", 0, 32))
+    if s:
+        cp(("fi", s, s + 1), ("rw", 32, 33))
+    emit("v", lambda: g.vector.tensor_copy(T.fw[:, 0:DUMP + 512].indirect(T.of16[:, 0:32]), A("jv", 0, 512)),
+         [("jv", 0, 512), ("of16", 0, 32)], [("fw", 0, DUMP + 512)])
+    tt(("fm", 0, 128), ("fw", 0, 128), ("mu", 0, 128), ALU.mult)
+    tt(("f2", 0, 64), ("fm", 0, 128, 2), ("fm", 1, 128, 2), ALU.add)
+    tt(("f4", 0, 32), ("f2", 0, 64, 2), ("f2", 1, 64, 2), ALU.add)
+    ts(("ls16", 0, 32), ("f4", 0, 32), ("pf", 2, 3), None, ALU.add)
+    pick("v", ("xg", 16, 272), "xb", 2064, "ls16", 0, 16)
+    pick("a", ("xg", 272, 528), "xb", 2064, "ls16", 16, 32)
+
+    if s:
+        cp(("vi", 0, s), ("msgin", 0, s))
+        ts(("fi", 0, s), ("vi", 0, s), 15, None, ALU.bitwise_and)
+        ts(("li", 0, s), ("vi", 0, s), 4, 15, ALU.logical_shift_right, ALU.bitwise_and)
+        ts(("ni", 0, s), ("vi", 0, s), 8, None, ALU.logical_shift_right)
+        tt(("qi", 0, s), ("fi", 1, s + 1), ("li", 0, s), ALU.is_equal)
+        tt(("df", 0, s), ("ni", 0, s), ("qi", 0, s), ALU.subtract)
+        if s == 1:
+            ts(("ei", 0, 1), ("df", 0, 1), ("col", 1, 2), None, ALU.add)
+        else:
+            if s == 3:
+                ts(("col", 3, 4), ("col", 1, 2), ("df", 2, 3), None, ALU.add)
+            ts(("ei", 0, 1), ("df", 0, 1), ("df", 1, 2), ("col", 3, 4) if s == 3 else ("col", 1, 2), ALU.add, ALU.add)
+    else:
+        cp(("ei", 0, 1), ("col", 1, 2))
+    ts(("ei", 1, 2), ("ei", 0, 1), 3, None, ALU.bitwise_and)
+    cp(("col", 4, 5), ("ei", 1, 2))
+    e3 = ("col", 4, 5)
+    ts(("sh16", 0, G), ("cf", 0, G), e3, 4.0, ALU.add, ALU.mult)
+    pick("v", ("sx", 0, 256), "xg", 560, "sh16", 0, 16)
+    pick("a", ("sx", 256, 4 * GT), "xg", 560, "sh16", 16, G)
+    quant("cq", "cz", OWN, "sx", 0, GT)
+
+    peers = [T.cores[(s + i) % N] for i in (1, 2, 3)]
+    eng = shared(core, peers)
+    q = len(eng) // 4
+    code_eng = [eng[0:2 * q], eng[2 * q:3 * q], eng[3 * q:4 * q]]
+    scale_eng = [eng[0:q], eng[q:2 * q], eng[2 * q:4 * q]]
+
+    def hop(cq, cz, width, src, land, rsem, lsem):
+        for codes in (True, False):
+            moves = []
+            for i in (1, 2, 3):
+                rid, pid, _ = topo.addr(peers[i - 1])
+                a, b = src(i), land(i)
+                if codes:
+                    x, y = A(cq, a, a + width).bitcast(dt.uint8), A(cq, b, b + width).bitcast(dt.uint8)
+                else:
+                    x, y = A(cz, a, a + width), A(cz, b, b + width)
+                moves.append(RemoteDMATransfer(dst_ids=[DstId(rid=rid, pnc=pid)], dma_engine_mask=sum(1 << e for e in (code_eng if codes else scale_eng)[i - 1]),
+                                               remote_sem=T.sem[rsem], srcs=[x], dsts=[y]))
+            lo, hi = src(1), src(3) + width
+            remote(lambda: g.remote_dma_fused(moves, local_sem=T.sem[lsem]), [(cq, lo, hi), (cz, lo, hi)], lsem, 4 * q)
+
+    hop("cq", "cz", G, lambda i: OWN + G * (i - 1), lambda i: LAND + G * (3 - i), "crecv", "cloc")
+    arrives("crecv", 8 * q, [("cq", LAND, LAND + 3 * G), ("cz", LAND, LAND + 3 * G)])
+
+    quant("aq", "az", 0, "ab", 0, 512)
+    quant("wq", "wz", 0, "wb", 0, 128)
+    mm("pwx", "wq", "wz", 0, "xq", "xz", 0, 512)
+    cp(("wx", 0, 512), ("pwx", 0, 512), "a")
+    quant("vq", "vz", 0, "vb", 0, 128)
+    ts(("lb0", 0, 32), ("lr", 0, 32), -1.0, 15.0, ALU.mult, ALU.add)
+    dma("s", "dl0", T.lb[0:1, :], T.lb0[0:16, :], [("lb0", 0, 32)], [])
+
+    for i in range(4):
+        mm("pa%d" % i, "aq", "az", 128 * i, "cq", "cz", OWN + 3 * G, GT)
+    for i in range(4):
+        o = ("hb", i, 4 * GT, 4)
+        r, w = [("pa%d" % i, 0, 512)], [("hb", i * 4 * GT, i * 4 * GT + 1)]
+        if i % 2 == 0:
+            emit("a", lambda: g.scalar.activation(ap(o), A("pa%d" % i, 0, GT), ACT.Relu, scale=0.05), r, w)
+        else:
+            emit("v", lambda: g.vector.tensor_scalar(ap(o), A("pa%d" % i, 0, GT), 0.0, 0.05, ALU.max, ALU.mult), r, w)
+    emit("v", lambda: g.vector.quantize_mx(A("hq", OWN, LAND), A("hz", OWN, LAND), A("hb", 0, 4 * GT)), [("hb", 0, 16 * GT)], [("hq", OWN, LAND), ("hz", OWN, LAND)])
+    hop("hq", "hz", GB, lambda i: OWN + G * i - 2, lambda i: LAND + GB * (i - 1), "hrecv", "hloc")
+    arrives("hrecv", 8 * q, [("hq", LAND, LAND + 3 * GB), ("hz", LAND, LAND + 3 * GB)])
+
+    mm("pv", "vq", "vz", 0, "hq", "hz", OWN, GT)
+    cp(("hv", 2, GB), ("pv", 0, G), "a")
+    cp(("hv", 0, 2), ("pv", GT - 2, GT), "a")
+    ts(("t1", 0, 16), ("u", 0, 16), ("pf", 6, 7), None, ALU.mult)
+    ts(("t2", 0, 16), ("u", 16, 32), ("pf", 4, 5), None, ALU.mult)
+    cp(("col", 5, 6), ("ei", 0, 1))
+    tt(("in2", 0, 16), ("t1", 0, 16), ("t2", 0, 16), ALU.add)
+    tt(("in2", 16, 32), ("t1", 0, 16), ("t2", 0, 16), ALU.add)
+    if s:
+        cp(("col", 6, 7), ("qi", s - 1, s))
+    tr(("ut", 0, 32), ("in2", 0, 32))
+    ts(("lb1", 0, 32), ("u", 0, 32), -1.0, ("col", 5, 6), ALU.mult, ALU.add)
+    dma("s", "dl1", T.lb[1:2, :], T.lb1[0:16, :], [("lb1", 0, 32)], [])
+    ts(("wi", 0, 32), ("ut", 0, 32), e3, 3.0, ALU.subtract, ALU.add)
+    ts(("zi", 0, 32), ("ut", 0, 32), e3, float(s + 4), ALU.subtract, ALU.add)
+    if s:
+        ts(("cm", 0, 32), ("ut", 0, 32), ("col", 1, 2), ("col", 6, 7), ALU.is_equal, ALU.mult)
+    ts(("ki", 0, 32), ("wi", 0, 32), 2, None, ALU.logical_shift_right)
+    ts(("bi", 0, 32), ("zi", 0, 32), 3, None, ALU.bitwise_and)
+    if s:
+        ts(("cm", 0, 32), ("cm", 0, 32), -1.0, 1.0, ALU.mult, ALU.add)
+    ts(("gf", 0, 32), ("ki", 0, 32), -1.0, float(G), ALU.mult, ALU.add)
+    ts(("bf", 0, 32), ("bi", 0, 32), float(GB), 1.0, ALU.mult, ALU.add)
+    if s:
+        tt(("gx", 0, 32), ("gf", 0, 32), ("cm", 0, 32), ALU.mult)
+    tt(("ix", 0, 32), ("gx" if s else "gf", 0, 32), ("bf", 0, 32), ALU.add)
+    for d in range(2):
+        cp(("ix16", d, 32, 2), ("ix", 16 * d, 16 * d + 16))
+
+    mm("pl0", "vq", "vz", 0, "hq", "hz", LAND + 3 * GB - 128, 128)
+    cp(("hv", GB, 4 * GB), ("pl0", 128 - 3 * GB, 128))
+    for k in range(2):
+        c = 256 * k
+        emit("v", lambda: g.vector.tensor_tensor(A("yb", c, c + 256), T.hv[:, 0:4 * GB].indirect(T.ix16[:, 16 * k:16 * k + 16]), A("wx", c, c + 256), ALU.add),
+             [("hv", 0, 4 * GB), ("ix16", 0, 32), ("wx", c, c + 256)], [("yb", c, c + 256)])
+        dma("s" if k == 0 else "a", "dy%d" % k, T.y[:, c:c + 256], A("yb", c, c + 256), [("yb", c, c + 256)], [])
+    finish()

@@ -9,102 +9,30 @@ GT = 4 * G
 GB = G + 2
 LAND = 144
 OWN = LAND - GT
+X0 = 16
+X1 = X0 + 512
 BIG = 1e25
 DUMP = 192
+ROUND4 = 50331648.0
 
-SCRATCH = {
-    "pb": ("sbuf", [128, 64], "bfloat16"),
-    "pt": ("sbuf", [128, 576], "bfloat16"),
-    "xb": ("sbuf", [128, 2064], "bfloat16"),
-    "ab": ("sbuf", [128, 2048], "bfloat16"),
-    "wb": ("sbuf", [128, 512], "bfloat16"),
-    "vb": ("sbuf", [128, 512], "bfloat16"),
-    "pq": ("sbuf", [128, 144], "float8_e4m3fn_x4"), "pz": ("sbuf", [128, 144], "uint8"),
-    "xq": ("sbuf", [128, 512], "float8_e4m3fn_x4"), "xz": ("sbuf", [128, 512], "uint8"),
-    "aq": ("sbuf", [128, 512], "float8_e4m3fn_x4"), "az": ("sbuf", [128, 512], "uint8"),
-    "wq": ("sbuf", [128, 128], "float8_e4m3fn_x4"), "wz": ("sbuf", [128, 128], "uint8"),
-    "vq": ("sbuf", [128, 128], "float8_e4m3fn_x4"), "vz": ("sbuf", [128, 128], "uint8"),
-    "cq": ("sbuf", [128, 256], "float8_e4m3fn_x4"), "cz": ("sbuf", [128, 256], "uint8"),
-    "hq": ("sbuf", [128, 256], "float8_e4m3fn_x4"), "hz": ("sbuf", [128, 256], "uint8"),
-    "sc": ("sbuf", [128, 256], "float32"),
-    "rs": ("sbuf", [128, 136], "float32"),
-    "xm": ("sbuf", [128, 264], "float32"),
-    "nn": ("sbuf", [128, 256], "bfloat16"),
-    "cc": ("sbuf", [128, 256], "bfloat16"),
-    "la": ("sbuf", [128, 32], "bfloat16"),
-    "lr": ("sbuf", [128, 32], "bfloat16"),
-    "eq": ("sbuf", [128, 32], "float32"),
-    "one": ("sbuf", [128, 32], "float32"),
-    "zb": ("sbuf", [128, 32], "bfloat16"),
-    "cnt": ("sbuf", [128, 32], "float32"),
-    "ncx": ("sbuf", [128, 32], "float32"),
-    "ex": ("sbuf", [128, 96], "bfloat16"),
-    "rw": ("sbuf", [128, 96], "bfloat16"),
-    "pr": ("sbuf", [128, 32], "float32"),
-    "pm": ("sbuf", [128, 32], "float32"),
-    "col": ("sbuf", [128, 16], "float32"),
-    "msg": ("sbuf", [128, 2], "uint16"),
-    "msgin": ("sbuf", [128, 4], "uint16"),
-    "pi": ("sbuf", [128, 8], "int32"),
-    "pf": ("sbuf", [128, 8], "float32"),
-    "row": ("sbuf", [128, 16], "float32"),
-    "mk": ("sbuf", [128, 32], "float32"),
-    "kd": ("sbuf", [128, 32], "float32"),
-    "mu": ("sbuf", [128, GT], "float32"),
-    "rt": ("sbuf", [128, GT], "float32"),
-    "rt2": ("sbuf", [128, GT // 2], "float32"),
-    "cf": ("sbuf", [128, G], "float32"),
-    "jv": ("sbuf", [128, 512], "float32"),
-    "u": ("sbuf", [128, 32], "float32"),
-    "nk": ("sbuf", [128, 32], "float32"),
-    "of": ("sbuf", [128, 32], "float32"),
-    "of16": ("sbuf", [128, 32], "uint16"),
-    "fw": ("sbuf", [128, DUMP + 512], "float32"),
-    "fm": ("sbuf", [128, 128], "float32"),
-    "f2": ("sbuf", [128, 64], "float32"),
-    "f4": ("sbuf", [128, 32], "float32"),
-    "ls16": ("sbuf", [128, 32], "uint16"),
-    "xg": ("sbuf", [128, 560], "bfloat16"),
-    "sh16": ("sbuf", [128, G], "uint16"),
-    "sx": ("sbuf", [128, 4 * GT], "bfloat16"),
-    "vi": ("sbuf", [128, 4], "int32"),
-    "fi": ("sbuf", [128, 4], "int32"),
-    "li": ("sbuf", [128, 4], "int32"),
-    "ni": ("sbuf", [128, 4], "int32"),
-    "qi": ("sbuf", [128, 4], "int32"),
-    "df": ("sbuf", [128, 4], "float32"),
-    "ei": ("sbuf", [128, 4], "int32"),
-    "hb": ("sbuf", [128, 4 * GT], "bfloat16"),
-    "t1": ("sbuf", [128, 16], "bfloat16"),
-    "t2": ("sbuf", [128, 16], "bfloat16"),
-    "in2": ("sbuf", [128, 32], "bfloat16"),
-    "ut": ("sbuf", [128, 32], "bfloat16"),
-    "wi": ("sbuf", [128, 32], "int32"),
-    "zi": ("sbuf", [128, 32], "int32"),
-    "bi": ("sbuf", [128, 32], "int32"),
-    "ki": ("sbuf", [128, 32], "int32"),
-    "gf": ("sbuf", [128, 32], "float32"),
-    "cm": ("sbuf", [128, 32], "float32"),
-    "gx": ("sbuf", [128, 32], "float32"),
-    "bf": ("sbuf", [128, 32], "float32"),
-    "ix": ("sbuf", [128, 32], "float32"),
-    "ix16": ("sbuf", [128, 32], "uint16"),
-    "hv": ("sbuf", [128, 4 * GB], "float32"),
-    "wx": ("sbuf", [128, 512], "float32"),
-    "yb": ("sbuf", [128, 512], "float32"),
-    "lb0": ("sbuf", [128, 32], "float32"),
-    "lb1": ("sbuf", [128, 32], "float32"),
-    "pl0": ("psum", [128, 512], "float32"),
-    "pl1": ("psum", [128, 512], "float32"),
-    "pwx": ("psum", [128, 512], "float32"),
-    "pa0": ("psum", [128, 512], "float32"),
-    "pa1": ("psum", [128, 512], "float32"),
-    "pa2": ("psum", [128, 512], "float32"),
-    "pa3": ("psum", [128, 512], "float32"),
-    "pv": ("psum", [128, 512], "float32"),
-}
-DMAS = ["dp", "dx0", "dx1", "dx2", "dx3", "da", "dw", "dv", "dl0", "dl1", "dy0", "dy1"]
-SEMAPHORES = ["sv", "sa", "st", "sg", "mrecv", "mloc", "crecv", "cloc", "hrecv", "hloc"] + DMAS
+SCRATCH = {}
+for _dtype, _names in {
+    "bfloat16": "pb 64 pt 576 xb 2064 ab 2048 wb 512 vb 512 nn 256 cc 256 la 32 lr 32 zb 32 ex 96 rw 96 msg 8 msgin 8 bn 16 bc 16 be 32 br 32 "
+                "xg 560 sx 544 hb 544 t1 16 t2 16 in2 32 ut 32",
+    "float32": "sc 256 rs 136 xm 264 eq 32 one 32 cnt 32 ncx 32 pr 32 pm 32 col 16 bs 32 bx 24 pf 8 row 16 mk 32 kd 32 mu 136 rt 136 rt2 68 cf 34 "
+               "jv 512 u 32 nk 32 of 32 fw 704 fm 128 f2 64 f4 32 gf 32 cm 32 gx 32 bf 32 ix 32 hv 144 wx 512 yb 512 lb0 32 lb1 32",
+    "int32": "pi 8 wi 32 zi 32 bi 32 ki 32",
+    "uint16": "of16 32 ls16 32 sh16 34 ix16 32",
+    "float8_e4m3fn_x4": "pq 144 xq 544 aq 512 wq 128 vq 128 cq 256 hq 256",
+    "uint8": "pz 144 xz 544 az 512 wz 128 vz 128 cz 256 hz 256",
+}.items():
+    _l = _names.split()
+    for _n, _w in zip(_l[::2], _l[1::2]):
+        SCRATCH[_n] = ("sbuf", [128, int(_w)], _dtype)
+for _n in ("pl0", "pl1", "pwx", "pa0", "pa1", "pa2", "pa3", "pv"):
+    SCRATCH[_n] = ("psum", [128, 512], "float32")
+SEMAPHORES = ["sv", "sa", "st", "sg", "lrecv", "rrecv", "bloc", "mrecv", "mloc", "crecv", "cloc", "hrecv", "hloc",
+              "dp", "dx0", "dx1", "dx2", "dx3", "da", "dw", "dv", "dl0", "dl1", "dy0", "dy1", "dy2"]
 
 
 def tracker(g, T):
@@ -199,6 +127,11 @@ def rank_program(g, core, T, topo):
         else:
             emit("a", lambda: g.scalar.activation(ap(o), ap(x), ACT.Copy), [span(x)], [span(o)])
 
+    def act(o, x, bias, scale=1.0):
+        r = [span(x)] + ([span(bias)] if isinstance(bias, tuple) else [])
+        b = ap(bias) if isinstance(bias, tuple) else bias
+        emit("a", lambda: g.scalar.activation(ap(o), ap(x), ACT.Identity, bias=b, scale=scale), r, [span(o)])
+
     def fill(o, c):
         emit("v", lambda: g.vector.memset(ap(o), c), [], [span(o)])
 
@@ -210,6 +143,9 @@ def rank_program(g, core, T, topo):
 
     def red(o, x, op):
         emit("v", lambda: g.vector.tensor_reduce(ap(o), ap(x), AxisListType.X, op), [span(x)], [span(o)])
+
+    def spread(o, x):
+        act(o, ("zb", 0, 32), x)
 
     def quant(cq, cz, a, src, b, n):
         emit("v", lambda: g.vector.quantize_mx(A(cq, a, a + n), A(cz, a, a + n), A(src, 4 * b, 4 * b + 4 * n)),
@@ -233,90 +169,136 @@ def rank_program(g, core, T, topo):
         else:
             emit("a", lambda: g.scalar.activation(ap(o), w, ACT.Copy), r, [span(o)])
 
+    def shared(src, dsts):
+        return [e for e in topo.engines(src, dsts[0]) if all(e in topo.engines(src, d) for d in dsts)]
+
+    def mask(engines):
+        return sum(1 << e for e in engines)
+
+    def where(d):
+        rid, pid, _ = topo.addr(d)
+        return DstId(rid=rid, pnc=pid)
+
     dma("a", "dp", A("pb", 0, 64), T.p[:, 0:64], [], [("pb", 0, 64)])
-    for k in range(4):
-        dma("s" if k % 2 == 0 else "a", "dx%d" % k, A("xb", 512 * k, 512 * k + 512), T.x[:, 512 * k:512 * k + 512], [], [("xb", 512 * k, 512 * k + 512)])
+    for k, que in ((0, "s"), (3, "a"), (1, "s"), (2, "a")):
+        dma(que, "dx%d" % k, A("xb", 512 * k, 512 * k + 512), T.x[:, 512 * k:512 * k + 512], [], [("xb", 512 * k, 512 * k + 512)])
     dma("s", "da", A("ab", 0, 2048), T.a[:, 0:2048], [], [("ab", 0, 2048)])
 
     iota(("pi", 0, 1), [[0, 1]], 0, 1)
     iota(("row", 0, 16), [[1, 16]], 0, 0)
-    iota(("kd", 0, 32), [[16, 32]], DUMP, 0)
     iota(("mu", 0, GT), [[0, G], [1, 4]], 0, 0)
-    for k in range(4):
-        iota(("rt", G * k, G * k + G), [[-4, G]], 4 * (G - 1) + (3 - (s + 1 + k) % N) + 1, 0)
-    iota(("jv", 0, 512), [[4, 32], [128, 16]], 0, 0)
+    first = [(3 - (s + 1 + k) % N) for k in range(4)]
+    k = 0
+    while k < 4:
+        n = 1
+        while k + n < 4 and first[k + n] == first[k + n - 1] - 1:
+            n += 1
+        iota(("rt", G * k, G * (k + n)), [[-1, n], [-4, G]], 4 * (G - 1) + first[k] + 1, 0)
+        k += n
+    iota(("kd", 0, 32), [[16, 32]], DUMP, 0)
+    iota(("jv", 0, 128), [[4, 8], [128, 16]], 0, 0)
+    fill(("zb", 0, 32), 0.0)
     fill(("pt", 0, 576), 0.0)
     fill(("rs", 0, 136), BIG)
     fill(("xm", 0, 1), -BIG)
+    fill(("bx", 0, 1), -BIG)
     fill(("rs", 0, 136, 16), -BIG)
-    fill(("eq", 0, 1), 0.0)
-    fill(("one", 0, 32), 1.0)
-    fill(("zb", 0, 32), 0.0)
-    fill(("pr", 16, 17), 0.0)
-    fill(("xb", 2048, 2064), 0.0)
-    fill(("xg", 0, 16), 0.0)
-    fill(("xg", 528, 560), 0.0)
-    fill(("fw", 0, 128), 2048.0)
+    cp(("eq", 0, 1), ("zb", 0, 1), "a")
+    cp(("pr", 16, 17), ("zb", 0, 1), "a")
+    act(("one", 0, 32), ("zb", 0, 32), 1.0)
+    cp(("xb", 2048, 2064), ("zb", 0, 16), "a")
+    cp(("xg", 0, 16), ("zb", 0, 16), "a")
+    cp(("xg", 528, 560), ("zb", 0, 32), "a")
     ts(("pi", 1, 2), ("pi", 0, 1), 15, None, ALU.bitwise_and)
     ts(("pi", 2, 3), ("pi", 0, 1), 3, None, ALU.bitwise_and)
     ts(("pi", 3, 4), ("pi", 0, 1), 2, 3, ALU.logical_shift_right, ALU.bitwise_and)
     ts(("pi", 4, 5), ("pi", 0, 1), 4, 1, ALU.logical_shift_right, ALU.bitwise_and)
     cp(("pf", 1, 5), ("pi", 1, 5))
-    ts(("pf", 5, 6), ("pf", 2, 3), 0.25, None, ALU.mult)
-    ts(("pf", 6, 7), ("pf", 4, 5), -1.0, 1.0, ALU.mult, ALU.add)
-    ts(("mk", 0, 16), ("row", 0, 16), ("pf", 1, 2), None, ALU.is_equal)
-    ts(("mk", 16, 32), ("row", 0, 16), ("pf", 1, 2), None, ALU.is_equal)
-    ts(("kd", 0, 32), ("kd", 0, 32), ("pf", 1, 2), None, ALU.add)
+    act(("pf", 5, 6), ("pf", 2, 3), 0.0, 0.25)
+    act(("pf", 6, 7), ("pf", 4, 5), 1.0, -1.0)
     ts(("mu", 0, GT), ("mu", 0, GT), ("pf", 3, 4), None, ALU.is_equal)
     tt(("rt", 0, GT), ("rt", 0, GT), ("mu", 0, GT), ALU.mult)
-    tt(("rt2", 0, GT // 2), ("rt", 0, GT, 2), ("rt", 1, GT, 2), ALU.add)
-    tt(("cf", 0, G), ("rt2", 0, GT // 2, 2), ("rt2", 1, GT // 2, 2), ALU.add)
-    ts(("cf", 0, G), ("cf", 0, G), ("pf", 5, 6), None, ALU.add)
     for k in range(4):
-        cp(("pt", 64 + 128 * k, 128 + 128 * k), ("pb", 0, 64))
+        cp(("pt", 64 + 128 * k, 128 + 128 * k), ("pb", 0, 64), "va"[k // 2])
     quant("pq", "pz", 0, "pt", 0, 144)
+    for k in (1, 2, 3):
+        act(("jv", 128 * k, 128 * k + 128), ("jv", 0, 128), 32.0 * k)
+    act(("fw", 0, 128), ("jv", 0, 128), 2048.0, 0.0)
+    act(("kd", 0, 32), ("kd", 0, 32), ("pf", 1, 2))
 
+    def border(d, a, za, b, zb, rsem):
+        e = shared(core, [d])
+        h = len(e) // 2
+        moves = [RemoteDMATransfer(dst_ids=[where(d)], dma_engine_mask=mask(e[:h]), remote_sem=T.sem[rsem],
+                                   srcs=[A("xq", a, a + 2).bitcast(dt.uint8)], dsts=[A("xq", b, b + 2).bitcast(dt.uint8)]),
+                 RemoteDMATransfer(dst_ids=[where(d)], dma_engine_mask=mask(e[h:]), remote_sem=T.sem[rsem],
+                                   srcs=[A("xz", za, za + 8)], dsts=[A("xz", zb, zb + 8)])]
+        remote(lambda: g.remote_dma_fused(moves, local_sem=T.sem.bloc), [("xq", a, a + 2), ("xz", za, za + 8)], "bloc", len(e))
+
+    def argmax(pl, c, n, bufs):
+        sc, xm, nn_, cc, o, w = bufs
+        return [lambda: tr((sc, o, o + n), (pl, c, c + n)),
+                lambda: scan((xm, o + 1, o + w + 1), (sc, o, o + w), ("rs", 1, w + 1), -BIG, ALU.max, ALU.min),
+                lambda: tt((nn_, o, o + w), (sc, o, o + w), (xm, o, o + w), ALU.is_le),
+                lambda: scan((cc, o, o + w), (nn_, o, o + w), (nn_, o, o + w), 0.0, ALU.mult, ALU.add)]
+
+    edge = ("bs", "bx", "bn", "bc", 0, 16)
+
+    quant("xq", "xz", X0, "xb", 0, 128)
+    if s > 0:
+        border(T.cores[s - 1], X0, X0, X1, X1, "rrecv")
+        arrives("lrecv", len(shared(T.cores[s - 1], [core])), [("xq", X0 - 2, X0), ("xz", X0 - 8, X0)])
+    quant("xq", "xz", X0 + 384, "xb", 384, 128)
+    if s < N - 1:
+        border(T.cores[s + 1], X1 - 2, X1 - 8, X0 - 2, X0 - 8, "lrecv")
+        arrives("rrecv", len(shared(T.cores[s + 1], [core])), [("xq", X1, X1 + 2), ("xz", X1, X1 + 8)])
+    tt(("rt2", 0, GT // 2), ("rt", 0, GT, 2), ("rt", 1, GT, 2), ALU.add)
+    ts(("mk", 0, 16), ("row", 0, 16), ("pf", 1, 2), None, ALU.is_equal)
+    tt(("cf", 0, G), ("rt2", 0, GT // 2, 2), ("rt2", 1, GT // 2, 2), ALU.add)
+    cp(("mk", 16, 32), ("mk", 0, 16), "a")
+    act(("cf", 0, G), ("cf", 0, G), ("pf", 5, 6))
     for P in range(2):
         pl = "pl%d" % P
-        for h in range(2):
-            c = 256 * P + 128 * h
-            quant("xq", "xz", c, "xb", c, 128)
-            mm(pl, "pq", "pz", 16 - 16 * h, "xq", "xz", c, 128, h == 0, h == 1)
+        c = 256 * P
+        quant("xq", "xz", X0 + (128, 256)[P], "xb", (128, 256)[P], 128)
+        for h in ((0, 1), (1, 0))[P]:
+            mm(pl, "pq", "pz", 16 - 16 * h, "xq", "xz", X0 + c + 128 * h, 128, h == P, h != P)
+        if P == 1 and s < N - 1:
+            mm("pwx", "pq", "pz", 16, "xq", "xz", X1 + 2 - 128, 128)
         o = 128 * P
-        tr(("sc", o, o + 128), (pl, 0, 128))
-        scan(("xm", o + 1, o + 129), ("sc", o, o + 128), ("rs", 1, 129), -BIG, ALU.max, ALU.min)
-        tt(("nn", o, o + 128), ("sc", o, o + 128), ("xm", o, o + 128), ALU.is_le)
-        scan(("cc", o, o + 128), ("nn", o, o + 128), ("nn", o, o + 128), 0.0, ALU.mult, ALU.add)
+        for f in argmax(pl, 0, 128, ("sc", "xm", "nn", "cc", o, 128)):
+            f()
         for h in range(2):
             for d in range(2):
                 b = 16 * d + 8 * P + 4 * h
                 cp(("la", b, b + 4), ("cc", o + 16 * h + 15, o + 128, 32), "v" if P == 1 and h == 0 else "a")
     tr(("lr", 0, 32), ("la", 0, 32))
 
-    for k, c in ((1, 0), (2, 31)):
-        emit("a", lambda: g.scalar.activation(A("ex", 32 * k, 32 * k + 32), A("zb", 0, 32), ACT.Identity, bias=A("lr", c, c + 1)),
-             [("zb", 0, 32), ("lr", c, c + 1)], [("ex", 32 * k, 32 * k + 32)])
+    right = argmax("pwx", 96, 32, edge) if s < N - 1 else [lambda: None] * 4
+    spread(("ex", 32, 64), ("lr", 0, 1))
+    spread(("ex", 64, 96), ("lr", 31, 32))
     tt(("eq", 1, 32), ("lr", 1, 32), ("lr", 0, 31), ALU.is_equal)
+    right[0]()
     scan(("cnt", 0, 32), ("one", 0, 32), ("eq", 0, 32), 0.0, ALU.add, ALU.subtract)
+    right[1]()
     ts(("ex", 0, 32), ("zb", 0, 32), ("cnt", 31, 32), None, ALU.add)
+    right[2]()
     tr(("rw", 0, 96), ("ex", 0, 96))
+    right[3]()
+    if s < N - 1:
+        spread(("be", 0, 32), ("bc", 15, 16))
+    act(("ncx", 0, 32), ("cnt", 0, 32), ("cnt", 31, 32), -1.0)
     tt(("pr", 17, 32), ("rw", 33, 48), ("rw", 64, 79), ALU.is_equal)
-    ts(("col", 0, 1), ("rw", 79, 80), 16.0, ("rw", 32, 33), ALU.mult, ALU.add)
+    if s < N - 1:
+        tr(("br", 0, 32), ("be", 0, 32))
     scan(("pr", 0, 16), ("rw", 0, 16), ("pr", 16, 32), 0.0, ALU.add, ALU.subtract)
     nn = ("pr", 15, 16)
     later = [T.cores[d] for d in range(s + 1, N)]
-
-    def shared(src, dsts):
-        return [e for e in topo.engines(src, dsts[0]) if all(e in topo.engines(src, d) for d in dsts)]
-
     if later:
-        ts(("msg", 0, 1), nn, 256.0, ("col", 0, 1), ALU.mult, ALU.add)
-        ids = []
-        for d in later:
-            rid, pid, _ = topo.addr(d)
-            ids.append(DstId(rid=rid, pnc=pid))
+        ts(("col", 7, 8), ("rw", 79, 80), ("br", 30, 31), None, ALU.is_equal)
+        ts(("msg", 0, 1), nn, ("col", 7, 8), None, ALU.subtract)
         eng = shared(core, later)
-        remote(lambda: g.remote_dma_fused([RemoteDMATransfer(dst_ids=ids, dma_engine_mask=sum(1 << e for e in eng), remote_sem=T.sem.mrecv,
+        remote(lambda: g.remote_dma_fused([RemoteDMATransfer(dst_ids=[where(d) for d in later], dma_engine_mask=mask(eng), remote_sem=T.sem.mrecv,
                                                              srcs=[A("msg", 0, 1)], dsts=[A("msgin", s, s + 1) for _ in later])],
                                           local_sem=T.sem.mloc), [("msg", 0, 1)], "mloc", len(eng))
     if s:
@@ -324,47 +306,40 @@ def rank_program(g, core, T, topo):
     dma("s", "dw", A("wb", 0, 512), T.w[:, 0:512], [("pr", 0, 16)], [("wb", 0, 512)])
     dma("s", "dv", A("vb", 0, 512), T.v[:, 0:512], [], [("vb", 0, 512)])
     tt(("pm", 0, 32), ("pr", 0, 32), ("mk", 0, 32), ALU.mult)
-    ts(("ncx", 0, 32), ("cnt", 0, 32), -1.0, ("cnt", 31, 32), ALU.mult, ALU.add)
     red(("eq", 0, 1), ("pm", 16, 32), ALU.add)
     red(("col", 2, 3), ("pm", 0, 16), ALU.add)
-    ts(("col", 1, 2), nn, -1.0, None, ALU.add)
+    act(("col", 1, 2), nn, -1.0)
+    act(("col", 8, 9), nn, -2.5)
     tt(("nk", 0, 32), ("eq", 0, 32), ("kd", 0, 32), ALU.mult)
     ts(("u", 0, 32), ("ncx", 0, 32), nn, ("col", 2, 3), ALU.add, ALU.subtract)
 
     tt(("of", 0, 32), ("u", 0, 32), ("nk", 0, 32), ALU.max)
     cp(("of16", 0, 32), ("of", 0, 32))
-    if s:
-        cp(("fi", s, s + 1), ("rw", 32, 33))
     emit("v", lambda: g.vector.tensor_copy(T.fw[:, 0:DUMP + 512].indirect(T.of16[:, 0:32]), A("jv", 0, 512)),
          [("jv", 0, 512), ("of16", 0, 32)], [("fw", 0, DUMP + 512)])
     tt(("fm", 0, 128), ("fw", 0, 128), ("mu", 0, 128), ALU.mult)
     tt(("f2", 0, 64), ("fm", 0, 128, 2), ("fm", 1, 128, 2), ALU.add)
     tt(("f4", 0, 32), ("f2", 0, 64, 2), ("f2", 1, 64, 2), ALU.add)
     ts(("ls16", 0, 32), ("f4", 0, 32), ("pf", 2, 3), None, ALU.add)
-    pick("v", ("xg", 16, 272), "xb", 2064, "ls16", 0, 16)
-    pick("a", ("xg", 272, 528), "xb", 2064, "ls16", 16, 32)
+    pick("a", ("xg", 304, 528), "xb", 2064, "ls16", 18, 32)
+    pick("v", ("xg", 16, 304), "xb", 2064, "ls16", 0, 18)
 
-    if s:
-        cp(("vi", 0, s), ("msgin", 0, s))
-        ts(("fi", 0, s), ("vi", 0, s), 15, None, ALU.bitwise_and)
-        ts(("li", 0, s), ("vi", 0, s), 4, 15, ALU.logical_shift_right, ALU.bitwise_and)
-        ts(("ni", 0, s), ("vi", 0, s), 8, None, ALU.logical_shift_right)
-        tt(("qi", 0, s), ("fi", 1, s + 1), ("li", 0, s), ALU.is_equal)
-        tt(("df", 0, s), ("ni", 0, s), ("qi", 0, s), ALU.subtract)
-        if s == 1:
-            ts(("ei", 0, 1), ("df", 0, 1), ("col", 1, 2), None, ALU.add)
-        else:
-            if s == 3:
-                ts(("col", 3, 4), ("col", 1, 2), ("df", 2, 3), None, ALU.add)
-            ts(("ei", 0, 1), ("df", 0, 1), ("df", 1, 2), ("col", 3, 4) if s == 3 else ("col", 1, 2), ALU.add, ALU.add)
+    E, ne3 = ("col", 5, 6), ("col", 9, 10)
+    if s == 0:
+        E = ("col", 1, 2)
+        ts(("col", 4, 5), nn, -2.5, ROUND4, ALU.add, ALU.add)
     else:
-        cp(("ei", 0, 1), ("col", 1, 2))
-    ts(("ei", 1, 2), ("ei", 0, 1), 3, None, ALU.bitwise_and)
-    cp(("col", 4, 5), ("ei", 1, 2))
-    e3 = ("col", 4, 5)
-    ts(("sh16", 0, G), ("cf", 0, G), e3, 4.0, ALU.add, ALU.mult)
-    pick("v", ("sx", 0, 256), "xg", 560, "sh16", 0, 16)
-    pick("a", ("sx", 256, 4 * GT), "xg", 560, "sh16", 16, G)
+        X = ("msgin", 0, 1) if s == 1 else ("col", 3, 4)
+        if s == 2:
+            ts(X, ("msgin", 0, 1), ("msgin", 1, 2), None, ALU.add)
+        if s == 3:
+            ts(X, ("msgin", 0, 1), ("msgin", 1, 2), ("msgin", 2, 3), ALU.add, ALU.add)
+        ts(("col", 4, 5), X, ("col", 8, 9), ROUND4, ALU.add, ALU.add)
+        ts(E, X, ("col", 1, 2), None, ALU.add)
+    ts(ne3, ("col", 4, 5), ROUND4, E, ALU.subtract, ALU.subtract)
+    ts(("sh16", 0, G), ("cf", 0, G), ne3, 4.0, ALU.subtract, ALU.mult)
+    pick("a", ("sx", 320, 4 * GT), "xg", 560, "sh16", 20, G)
+    pick("v", ("sx", 0, 320), "xg", 560, "sh16", 0, 20)
     quant("cq", "cz", OWN, "sx", 0, GT)
 
     peers = [T.cores[(s + i) % N] for i in (1, 2, 3)]
@@ -377,13 +352,12 @@ def rank_program(g, core, T, topo):
         for codes in (True, False):
             moves = []
             for i in (1, 2, 3):
-                rid, pid, _ = topo.addr(peers[i - 1])
                 a, b = src(i), land(i)
                 if codes:
                     x, y = A(cq, a, a + width).bitcast(dt.uint8), A(cq, b, b + width).bitcast(dt.uint8)
                 else:
                     x, y = A(cz, a, a + width), A(cz, b, b + width)
-                moves.append(RemoteDMATransfer(dst_ids=[DstId(rid=rid, pnc=pid)], dma_engine_mask=sum(1 << e for e in (code_eng if codes else scale_eng)[i - 1]),
+                moves.append(RemoteDMATransfer(dst_ids=[where(peers[i - 1])], dma_engine_mask=mask((code_eng if codes else scale_eng)[i - 1]),
                                                remote_sem=T.sem[rsem], srcs=[x], dsts=[y]))
             lo, hi = src(1), src(3) + width
             remote(lambda: g.remote_dma_fused(moves, local_sem=T.sem[lsem]), [(cq, lo, hi), (cz, lo, hi)], lsem, 4 * q)
@@ -393,11 +367,22 @@ def rank_program(g, core, T, topo):
 
     quant("aq", "az", 0, "ab", 0, 512)
     quant("wq", "wz", 0, "wb", 0, 128)
-    mm("pwx", "wq", "wz", 0, "xq", "xz", 0, 512)
+    mm("pwx", "wq", "wz", 0, "xq", "xz", X0, 512)
     cp(("wx", 0, 512), ("pwx", 0, 512), "a")
     quant("vq", "vz", 0, "vb", 0, 128)
+    ts(("t1", 0, 16), ("u", 0, 16), ("pf", 6, 7), None, ALU.mult)
+    ts(("t2", 0, 16), ("u", 16, 32), ("pf", 4, 5), None, ALU.mult)
     ts(("lb0", 0, 32), ("lr", 0, 32), -1.0, 15.0, ALU.mult, ALU.add)
+    tt(("in2", 0, 16), ("t1", 0, 16), ("t2", 0, 16), ALU.add)
+    tt(("in2", 16, 32), ("t1", 0, 16), ("t2", 0, 16), ALU.add)
+    ts(("lb1", 0, 32), ("u", 0, 32), -1.0, E, ALU.mult, ALU.add)
+    tr(("ut", 0, 32), ("in2", 0, 32))
     dma("s", "dl0", T.lb[0:1, :], T.lb0[0:16, :], [("lb0", 0, 32)], [])
+    dma("s", "dl1", T.lb[1:2, :], T.lb1[0:16, :], [("lb1", 0, 32)], [])
+    left = [lambda: None] * 4
+    if s:
+        mm("pl1", "pq", "pz", 16, "xq", "xz", X0 - 2, 128)
+        left = argmax("pl1", 0, 32, edge)
 
     for i in range(4):
         mm("pa%d" % i, "aq", "az", 128 * i, "cq", "cz", OWN + 3 * G, GT)
@@ -415,27 +400,23 @@ def rank_program(g, core, T, topo):
     mm("pv", "vq", "vz", 0, "hq", "hz", OWN, GT)
     cp(("hv", 2, GB), ("pv", 0, G), "a")
     cp(("hv", 0, 2), ("pv", GT - 2, GT), "a")
-    ts(("t1", 0, 16), ("u", 0, 16), ("pf", 6, 7), None, ALU.mult)
-    ts(("t2", 0, 16), ("u", 16, 32), ("pf", 4, 5), None, ALU.mult)
-    cp(("col", 5, 6), ("ei", 0, 1))
-    tt(("in2", 0, 16), ("t1", 0, 16), ("t2", 0, 16), ALU.add)
-    tt(("in2", 16, 32), ("t1", 0, 16), ("t2", 0, 16), ALU.add)
-    if s:
-        cp(("col", 6, 7), ("qi", s - 1, s))
-    tr(("ut", 0, 32), ("in2", 0, 32))
-    ts(("lb1", 0, 32), ("u", 0, 32), -1.0, ("col", 5, 6), ALU.mult, ALU.add)
-    dma("s", "dl1", T.lb[1:2, :], T.lb1[0:16, :], [("lb1", 0, 32)], [])
-    ts(("wi", 0, 32), ("ut", 0, 32), e3, 3.0, ALU.subtract, ALU.add)
-    ts(("zi", 0, 32), ("ut", 0, 32), e3, float(s + 4), ALU.subtract, ALU.add)
-    if s:
-        ts(("cm", 0, 32), ("ut", 0, 32), ("col", 1, 2), ("col", 6, 7), ALU.is_equal, ALU.mult)
+    left[0]()
+    ts(("wi", 0, 32), ("ut", 0, 32), ne3, 3.0, ALU.add, ALU.add)
+    left[1]()
+    ts(("zi", 0, 32), ("ut", 0, 32), ne3, float(s + 4), ALU.add, ALU.add)
+    left[2]()
     ts(("ki", 0, 32), ("wi", 0, 32), 2, None, ALU.logical_shift_right)
-    ts(("bi", 0, 32), ("zi", 0, 32), 3, None, ALU.bitwise_and)
+    left[3]()
     if s:
-        ts(("cm", 0, 32), ("cm", 0, 32), -1.0, 1.0, ALU.mult, ALU.add)
+        spread(("be", 0, 32), ("bc", 15, 16))
+    ts(("bi", 0, 32), ("zi", 0, 32), 3, None, ALU.bitwise_and)
     ts(("gf", 0, 32), ("ki", 0, 32), -1.0, float(G), ALU.mult, ALU.add)
     ts(("bf", 0, 32), ("bi", 0, 32), float(GB), 1.0, ALU.mult, ALU.add)
     if s:
+        tr(("br", 0, 32), ("be", 0, 32))
+        ts(("col", 6, 7), ("br", 1, 2), ("rw", 32, 33), None, ALU.is_equal)
+        ts(("cm", 0, 32), ("ut", 0, 32), ("col", 1, 2), ("col", 6, 7), ALU.is_equal, ALU.mult)
+        ts(("cm", 0, 32), ("cm", 0, 32), -1.0, 1.0, ALU.mult, ALU.add)
         tt(("gx", 0, 32), ("gf", 0, 32), ("cm", 0, 32), ALU.mult)
     tt(("ix", 0, 32), ("gx" if s else "gf", 0, 32), ("bf", 0, 32), ALU.add)
     for d in range(2):
@@ -443,9 +424,8 @@ def rank_program(g, core, T, topo):
 
     mm("pl0", "vq", "vz", 0, "hq", "hz", LAND + 3 * GB - 128, 128)
     cp(("hv", GB, 4 * GB), ("pl0", 128 - 3 * GB, 128))
-    for k in range(2):
-        c = 256 * k
-        emit("v", lambda: g.vector.tensor_tensor(A("yb", c, c + 256), T.hv[:, 0:4 * GB].indirect(T.ix16[:, 16 * k:16 * k + 16]), A("wx", c, c + 256), ALU.add),
-             [("hv", 0, 4 * GB), ("ix16", 0, 32), ("wx", c, c + 256)], [("yb", c, c + 256)])
-        dma("s" if k == 0 else "a", "dy%d" % k, T.y[:, c:c + 256], A("yb", c, c + 256), [("yb", c, c + 256)], [])
+    for k, (c, d) in enumerate(((0, 160), (160, 352), (352, 512))):
+        emit("v", lambda: g.vector.tensor_tensor(A("yb", c, d), T.hv[:, 0:4 * GB].indirect(T.ix16[:, c // 16:d // 16]), A("wx", c, d), ALU.add),
+             [("hv", 0, 4 * GB), ("ix16", 0, 32), ("wx", c, d)], [("yb", c, d)])
+        dma("sas"[k], "dy%d" % k, T.y[:, c:d], A("yb", c, d), [("yb", c, d)], [])
     finish()

@@ -4,11 +4,10 @@ from concourse.mybir import dt, AluOpType, AxisListType, ActivationFunctionType
 ALU = AluOpType
 ACT = ActivationFunctionType
 N = 4
-G = 34
+G = 36
 GT = 4 * G
 GB = G + 2
-LAND = 144
-OWN = LAND - GT
+LAND = GT
 X0 = 16
 X1 = X0 + 512
 BIG = 1e25
@@ -17,14 +16,14 @@ ROUND4 = 50331648.0
 
 SCRATCH = {}
 for _dtype, _names in {
-    "bfloat16": "pb 64 pt 576 xb 2064 ab 2048 wb 512 vb 512 nn 256 cc 256 la 32 lr 32 zb 32 ex 96 rw 96 msg 8 msgin 8 bn 16 bc 16 be 32 br 32 "
-                "xg 560 sx 544 hb 544 t1 16 t2 16 in2 32 ut 32",
-    "float32": "sc 256 rs 136 xm 264 eq 32 one 32 cnt 32 ncx 32 pr 32 pm 32 col 16 bs 32 bx 24 pf 8 row 16 mk 32 kd 32 mu 136 rt 136 rt2 68 cf 34 "
-               "jv 512 u 32 nk 32 of 32 fw 704 fm 128 f2 64 f4 32 gf 32 cm 32 gx 32 bf 32 ix 32 hv 144 wx 512 yb 512 lb0 32 lb1 32",
+    "bfloat16": "pb 64 pt 576 xb 2048 ab 2048 wb 512 vb 512 nn 256 cc 256 la 32 lr 32 zb 32 ex 96 rw 96 msg 8 msgin 8 bn 16 bc 16 "
+                "xg 592 sx 576 hb 576 t1 16 t2 16 in2 32 ut 32",
+    "float32": "sc 256 rs 136 xm 264 eq 32 one 32 cnt 32 ncx 32 pr 32 pm 32 col 16 bs 32 bx 24 be 32 br 32 pf 8 pg 8 row 16 mk 32 kd 32 mu 128 "
+               "mb 128 rt 36 cf 36 cfe 36 jv 512 u 32 nk 32 of 32 fw 704 fm 128 gf 32 cm 32 gx 32 bf 32 ix 32 hv 152 wx 512 yb 512 lb0 32 lb1 32",
     "int32": "pi 8 wi 32 zi 32 bi 32 ki 32",
-    "uint16": "of16 32 ls16 32 sh16 34 ix16 32",
-    "float8_e4m3fn_x4": "pq 144 xq 544 aq 512 wq 128 vq 128 cq 256 hq 256",
-    "uint8": "pz 144 xz 544 az 512 wz 128 vz 128 cz 256 hz 256",
+    "uint16": "of16 32 ls16 32 sh16 36 ix16 32",
+    "float8_e4m3fn_x4": "pq 144 xq 544 aq 512 wq 128 vq 128 cq 272 hq 272",
+    "uint8": "pz 144 xz 544 az 512 wz 128 vz 128 cz 272 hz 272",
 }.items():
     _l = _names.split()
     for _n, _w in zip(_l[::2], _l[1::2]):
@@ -155,7 +154,7 @@ def rank_program(g, core, T, topo):
         emit("t", lambda: g.tensor.matmul_mx(A(o, 0, n), A(lq, a, a + 128), A(lz, a, a + 128), A(rq, b, b + n), A(rz, b, b + n), start, stop),
              [(lq, a, a + 128), (lz, a, a + 128), (rq, b, b + n), (rz, b, b + n)], [(o, 0, 512)], chain=not start)
 
-    def iota(o, pattern, base, cm):
+    def iota(o, pattern, base, cm=0):
         if o[0] == "pi":
             emit("g", lambda: g.iota(ap(o), pattern, base, cm), [], [span(o)])
         else:
@@ -185,18 +184,18 @@ def rank_program(g, core, T, topo):
     dma("s", "da", A("ab", 0, 2048), T.a[:, 0:2048], [], [("ab", 0, 2048)])
 
     iota(("pi", 0, 1), [[0, 1]], 0, 1)
-    iota(("row", 0, 16), [[1, 16]], 0, 0)
-    iota(("mu", 0, GT), [[0, G], [1, 4]], 0, 0)
+    iota(("mu", 0, 128), [[0, 32], [1, 4]], 0)
+    iota(("row", 0, 16), [[1, 16]], 0)
     first = [(3 - (s + 1 + k) % N) for k in range(4)]
     k = 0
     while k < 4:
         n = 1
         while k + n < 4 and first[k + n] == first[k + n - 1] - 1:
             n += 1
-        iota(("rt", G * k, G * (k + n)), [[-1, n], [-4, G]], 4 * (G - 1) + first[k] + 1, 0)
+        iota(("rt", G // 4 * k, G // 4 * (k + n)), [[-1, n], [-16, G // 4]], 4 * (G - 1) + first[k] + 1)
         k += n
-    iota(("kd", 0, 32), [[16, 32]], DUMP, 0)
-    iota(("jv", 0, 128), [[4, 8], [128, 16]], 0, 0)
+    iota(("kd", 0, 32), [[16, 32]], DUMP)
+    iota(("jv", 0, 128), [[4, 8], [128, 16]], 0)
     fill(("zb", 0, 32), 0.0)
     fill(("pt", 0, 576), 0.0)
     fill(("rs", 0, 136), BIG)
@@ -206,25 +205,29 @@ def rank_program(g, core, T, topo):
     cp(("eq", 0, 1), ("zb", 0, 1), "a")
     cp(("pr", 16, 17), ("zb", 0, 1), "a")
     act(("one", 0, 32), ("zb", 0, 32), 1.0)
-    cp(("xb", 2048, 2064), ("zb", 0, 16), "a")
     cp(("xg", 0, 16), ("zb", 0, 16), "a")
     cp(("xg", 528, 560), ("zb", 0, 32), "a")
+    cp(("xg", 560, 592), ("zb", 0, 32), "a")
     ts(("pi", 1, 2), ("pi", 0, 1), 15, None, ALU.bitwise_and)
     ts(("pi", 2, 3), ("pi", 0, 1), 3, None, ALU.bitwise_and)
     ts(("pi", 3, 4), ("pi", 0, 1), 2, 3, ALU.logical_shift_right, ALU.bitwise_and)
     ts(("pi", 4, 5), ("pi", 0, 1), 4, 1, ALU.logical_shift_right, ALU.bitwise_and)
     cp(("pf", 1, 5), ("pi", 1, 5))
-    act(("pf", 5, 6), ("pf", 2, 3), 0.0, 0.25)
-    act(("pf", 6, 7), ("pf", 4, 5), 1.0, -1.0)
-    ts(("mu", 0, GT), ("mu", 0, GT), ("pf", 3, 4), None, ALU.is_equal)
-    tt(("rt", 0, GT), ("rt", 0, GT), ("mu", 0, GT), ALU.mult)
+    p16, p4, pd4, pd16 = [("pf", k, k + 1) for k in (1, 2, 3, 4)]
+    ts(("mb", 0, 128), ("mu", 0, 128), pd4, -BIG, ALU.is_equal, ALU.mult)
+    ts(("mk", 0, 16), ("row", 0, 16), p16, None, ALU.is_equal)
     for k in range(4):
         cp(("pt", 64 + 128 * k, 128 + 128 * k), ("pb", 0, 64), "va"[k // 2])
     quant("pq", "pz", 0, "pt", 0, 144)
+    act(("pg", 0, 1), p4, 0.0, 0.25)
+    act(("pg", 1, 2), pd16, 1.0, -1.0)
+    act(("pg", 2, 3), pd4, ("pg", 0, 1), -4.0)
+    cp(("mk", 16, 32), ("mk", 0, 16), "a")
     for k in (1, 2, 3):
         act(("jv", 128 * k, 128 * k + 128), ("jv", 0, 128), 32.0 * k)
-    act(("fw", 0, 128), ("jv", 0, 128), 2048.0, 0.0)
-    act(("kd", 0, 32), ("kd", 0, 32), ("pf", 1, 2))
+    act(("fw", 0, 128), ("jv", 0, 128), 0.0, 0.0)
+    act(("kd", 0, 32), ("kd", 0, 32), p16)
+    act(("cf", 0, G), ("rt", 0, G), ("pg", 2, 3))
 
     def border(d, a, za, b, zb, rsem):
         e = shared(core, [d])
@@ -244,33 +247,25 @@ def rank_program(g, core, T, topo):
 
     edge = ("bs", "bx", "bn", "bc", 0, 16)
 
-    quant("xq", "xz", X0, "xb", 0, 128)
-    if s > 0:
-        border(T.cores[s - 1], X0, X0, X1, X1, "rrecv")
-        arrives("lrecv", len(shared(T.cores[s - 1], [core])), [("xq", X0 - 2, X0), ("xz", X0 - 8, X0)])
-    quant("xq", "xz", X0 + 384, "xb", 384, 128)
-    if s < N - 1:
-        border(T.cores[s + 1], X1 - 2, X1 - 8, X0 - 2, X0 - 8, "lrecv")
-        arrives("rrecv", len(shared(T.cores[s + 1], [core])), [("xq", X1, X1 + 2), ("xz", X1, X1 + 8)])
-    tt(("rt2", 0, GT // 2), ("rt", 0, GT, 2), ("rt", 1, GT, 2), ALU.add)
-    ts(("mk", 0, 16), ("row", 0, 16), ("pf", 1, 2), None, ALU.is_equal)
-    tt(("cf", 0, G), ("rt2", 0, GT // 2, 2), ("rt2", 1, GT // 2, 2), ALU.add)
-    cp(("mk", 16, 32), ("mk", 0, 16), "a")
-    act(("cf", 0, G), ("cf", 0, G), ("pf", 5, 6))
-    for P in range(2):
+    for P, quarters in enumerate(((0, 3), (1, 2))):
         pl = "pl%d" % P
-        c = 256 * P
-        quant("xq", "xz", X0 + (128, 256)[P], "xb", (128, 256)[P], 128)
-        for h in ((0, 1), (1, 0))[P]:
-            mm(pl, "pq", "pz", 16 - 16 * h, "xq", "xz", X0 + c + 128 * h, 128, h == P, h != P)
+        for h, c in enumerate(quarters):
+            quant("xq", "xz", X0 + 128 * c, "xb", 128 * c, 128)
+            if c == 0 and s > 0:
+                border(T.cores[s - 1], X0, X0, X1, X1, "rrecv")
+                arrives("lrecv", len(shared(T.cores[s - 1], [core])), [("xq", X0 - 2, X0), ("xz", X0 - 8, X0)])
+            if c == 3 and s < N - 1:
+                border(T.cores[s + 1], X1 - 2, X1 - 8, X0 - 2, X0 - 8, "lrecv")
+                arrives("rrecv", len(shared(T.cores[s + 1], [core])), [("xq", X1, X1 + 2), ("xz", X1, X1 + 8)])
+            mm(pl, "pq", "pz", 16 - 16 * h, "xq", "xz", X0 + 128 * c, 128, h == 0, h == 1)
         if P == 1 and s < N - 1:
             mm("pwx", "pq", "pz", 16, "xq", "xz", X1 + 2 - 128, 128)
         o = 128 * P
         for f in argmax(pl, 0, 128, ("sc", "xm", "nn", "cc", o, 128)):
             f()
-        for h in range(2):
+        for h, c in enumerate(quarters):
             for d in range(2):
-                b = 16 * d + 8 * P + 4 * h
+                b = 16 * d + 4 * c
                 cp(("la", b, b + 4), ("cc", o + 16 * h + 15, o + 128, 32), "v" if P == 1 and h == 0 else "a")
     tr(("lr", 0, 32), ("la", 0, 32))
 
@@ -285,18 +280,17 @@ def rank_program(g, core, T, topo):
     right[2]()
     tr(("rw", 0, 96), ("ex", 0, 96))
     right[3]()
-    if s < N - 1:
+    later = [T.cores[d] for d in range(s + 1, N)]
+    if later:
         spread(("be", 0, 32), ("bc", 15, 16))
     act(("ncx", 0, 32), ("cnt", 0, 32), ("cnt", 31, 32), -1.0)
     tt(("pr", 17, 32), ("rw", 33, 48), ("rw", 64, 79), ALU.is_equal)
-    if s < N - 1:
+    if later:
         tr(("br", 0, 32), ("be", 0, 32))
     scan(("pr", 0, 16), ("rw", 0, 16), ("pr", 16, 32), 0.0, ALU.add, ALU.subtract)
     nn = ("pr", 15, 16)
-    later = [T.cores[d] for d in range(s + 1, N)]
     if later:
-        ts(("col", 7, 8), ("rw", 79, 80), ("br", 30, 31), None, ALU.is_equal)
-        ts(("msg", 0, 1), nn, ("col", 7, 8), None, ALU.subtract)
+        ts(("msg", 0, 1), ("rw", 79, 80), ("br", 30, 31), nn, ALU.is_equal, ALU.subtract)
         eng = shared(core, later)
         remote(lambda: g.remote_dma_fused([RemoteDMATransfer(dst_ids=[where(d) for d in later], dma_engine_mask=mask(eng), remote_sem=T.sem.mrecv,
                                                              srcs=[A("msg", 0, 1)], dsts=[A("msgin", s, s + 1) for _ in later])],
@@ -309,7 +303,8 @@ def rank_program(g, core, T, topo):
     red(("eq", 0, 1), ("pm", 16, 32), ALU.add)
     red(("col", 2, 3), ("pm", 0, 16), ALU.add)
     act(("col", 1, 2), nn, -1.0)
-    act(("col", 8, 9), nn, -2.5)
+    act(("col", 8, 9), nn, 2.5, -1.0)
+    act(("cfe", 0, G), ("cf", 0, G), ("col", 1, 2))
     tt(("nk", 0, 32), ("eq", 0, 32), ("kd", 0, 32), ALU.mult)
     ts(("u", 0, 32), ("ncx", 0, 32), nn, ("col", 2, 3), ALU.add, ALU.subtract)
 
@@ -317,30 +312,28 @@ def rank_program(g, core, T, topo):
     cp(("of16", 0, 32), ("of", 0, 32))
     emit("v", lambda: g.vector.tensor_copy(T.fw[:, 0:DUMP + 512].indirect(T.of16[:, 0:32]), A("jv", 0, 512)),
          [("jv", 0, 512), ("of16", 0, 32)], [("fw", 0, DUMP + 512)])
-    tt(("fm", 0, 128), ("fw", 0, 128), ("mu", 0, 128), ALU.mult)
-    tt(("f2", 0, 64), ("fm", 0, 128, 2), ("fm", 1, 128, 2), ALU.add)
-    tt(("f4", 0, 32), ("f2", 0, 64, 2), ("f2", 1, 64, 2), ALU.add)
-    ts(("ls16", 0, 32), ("f4", 0, 32), ("pf", 2, 3), None, ALU.add)
-    pick("a", ("xg", 304, 528), "xb", 2064, "ls16", 18, 32)
-    pick("v", ("xg", 16, 304), "xb", 2064, "ls16", 0, 18)
+    scan(("fm", 0, 128), ("mb", 0, 128), ("fw", 0, 128), 0.0, ALU.add, ALU.max)
+    ts(("ls16", 0, 32), ("fm", 3, 128, 4), p4, None, ALU.add)
+    pick("a", ("xg", 304, 528), "xb", 2048, "ls16", 18, 32)
+    pick("v", ("xg", 16, 304), "xb", 2048, "ls16", 0, 18)
 
-    E, ne3 = ("col", 5, 6), ("col", 9, 10)
+    E, z, ne3 = ("col", 5, 6), ("col", 10, 11), ("col", 9, 10)
+    Y = 0.0
     if s == 0:
         E = ("col", 1, 2)
-        ts(("col", 4, 5), nn, -2.5, ROUND4, ALU.add, ALU.add)
+        ts(("col", 4, 5), ("col", 8, 9), ROUND4, None, ALU.add)
     else:
-        X = ("msgin", 0, 1) if s == 1 else ("col", 3, 4)
+        Y = ("msgin", 0, 1) if s == 1 else ("col", 3, 4)
         if s == 2:
-            ts(X, ("msgin", 0, 1), ("msgin", 1, 2), None, ALU.add)
+            ts(Y, ("msgin", 0, 1), ("msgin", 1, 2), None, ALU.add)
         if s == 3:
-            ts(X, ("msgin", 0, 1), ("msgin", 1, 2), ("msgin", 2, 3), ALU.add, ALU.add)
-        ts(("col", 4, 5), X, ("col", 8, 9), ROUND4, ALU.add, ALU.add)
-        ts(E, X, ("col", 1, 2), None, ALU.add)
-    ts(ne3, ("col", 4, 5), ROUND4, E, ALU.subtract, ALU.subtract)
-    ts(("sh16", 0, G), ("cf", 0, G), ne3, 4.0, ALU.subtract, ALU.mult)
-    pick("a", ("sx", 320, 4 * GT), "xg", 560, "sh16", 20, G)
-    pick("v", ("sx", 0, 320), "xg", 560, "sh16", 0, 20)
-    quant("cq", "cz", OWN, "sx", 0, GT)
+            ts(Y, ("msgin", 0, 1), ("msgin", 1, 2), ("msgin", 2, 3), ALU.add, ALU.add)
+        ts(("col", 4, 5), Y, ("col", 8, 9), ROUND4, ALU.add, ALU.add)
+    ts(z, ("col", 4, 5), ROUND4, Y, ALU.subtract, ALU.subtract)
+    ts(("sh16", 0, G), ("cfe", 0, G), z, 4.0, ALU.add, ALU.mult)
+    pick("a", ("sx", 320, 4 * GT), "xg", 592, "sh16", 20, G)
+    pick("v", ("sx", 0, 320), "xg", 592, "sh16", 0, 20)
+    quant("cq", "cz", 0, "sx", 0, GT)
 
     peers = [T.cores[(s + i) % N] for i in (1, 2, 3)]
     eng = shared(core, peers)
@@ -362,7 +355,7 @@ def rank_program(g, core, T, topo):
             lo, hi = src(1), src(3) + width
             remote(lambda: g.remote_dma_fused(moves, local_sem=T.sem[lsem]), [(cq, lo, hi), (cz, lo, hi)], lsem, 4 * q)
 
-    hop("cq", "cz", G, lambda i: OWN + G * (i - 1), lambda i: LAND + G * (3 - i), "crecv", "cloc")
+    hop("cq", "cz", G, lambda i: G * (i - 1), lambda i: LAND + G * (3 - i), "crecv", "cloc")
     arrives("crecv", 8 * q, [("cq", LAND, LAND + 3 * G), ("cz", LAND, LAND + 3 * G)])
 
     quant("aq", "az", 0, "ab", 0, 512)
@@ -370,13 +363,16 @@ def rank_program(g, core, T, topo):
     mm("pwx", "wq", "wz", 0, "xq", "xz", X0, 512)
     cp(("wx", 0, 512), ("pwx", 0, 512), "a")
     quant("vq", "vz", 0, "vb", 0, 128)
-    ts(("t1", 0, 16), ("u", 0, 16), ("pf", 6, 7), None, ALU.mult)
-    ts(("t2", 0, 16), ("u", 16, 32), ("pf", 4, 5), None, ALU.mult)
-    ts(("lb0", 0, 32), ("lr", 0, 32), -1.0, 15.0, ALU.mult, ALU.add)
+    ts(("t1", 0, 16), ("u", 0, 16), ("pg", 1, 2), None, ALU.mult)
+    ts(("t2", 0, 16), ("u", 16, 32), pd16, None, ALU.mult)
+    if s:
+        ts(E, Y, -1.0, ("col", 1, 2), ALU.mult, ALU.add)
+    ts(ne3, z, -1.0, ("col", 1, 2), ALU.mult, ALU.subtract)
     tt(("in2", 0, 16), ("t1", 0, 16), ("t2", 0, 16), ALU.add)
     tt(("in2", 16, 32), ("t1", 0, 16), ("t2", 0, 16), ALU.add)
     ts(("lb1", 0, 32), ("u", 0, 32), -1.0, E, ALU.mult, ALU.add)
     tr(("ut", 0, 32), ("in2", 0, 32))
+    act(("lb0", 0, 32), ("lr", 0, 32), 15.0, -1.0)
     dma("s", "dl0", T.lb[0:1, :], T.lb0[0:16, :], [("lb0", 0, 32)], [])
     dma("s", "dl1", T.lb[1:2, :], T.lb1[0:16, :], [("lb1", 0, 32)], [])
     left = [lambda: None] * 4
@@ -385,7 +381,7 @@ def rank_program(g, core, T, topo):
         left = argmax("pl1", 0, 32, edge)
 
     for i in range(4):
-        mm("pa%d" % i, "aq", "az", 128 * i, "cq", "cz", OWN + 3 * G, GT)
+        mm("pa%d" % i, "aq", "az", 128 * i, "cq", "cz", 3 * G, GT)
     for i in range(4):
         o = ("hb", i, 4 * GT, 4)
         r, w = [("pa%d" % i, 0, 512)], [("hb", i * 4 * GT, i * 4 * GT + 1)]
@@ -393,11 +389,11 @@ def rank_program(g, core, T, topo):
             emit("a", lambda: g.scalar.activation(ap(o), A("pa%d" % i, 0, GT), ACT.Relu, scale=0.05), r, w)
         else:
             emit("v", lambda: g.vector.tensor_scalar(ap(o), A("pa%d" % i, 0, GT), 0.0, 0.05, ALU.max, ALU.mult), r, w)
-    emit("v", lambda: g.vector.quantize_mx(A("hq", OWN, LAND), A("hz", OWN, LAND), A("hb", 0, 4 * GT)), [("hb", 0, 16 * GT)], [("hq", OWN, LAND), ("hz", OWN, LAND)])
-    hop("hq", "hz", GB, lambda i: OWN + G * i - 2, lambda i: LAND + GB * (i - 1), "hrecv", "hloc")
+    emit("v", lambda: g.vector.quantize_mx(A("hq", 0, GT), A("hz", 0, GT), A("hb", 0, 4 * GT)), [("hb", 0, 16 * GT)], [("hq", 0, GT), ("hz", 0, GT)])
+    hop("hq", "hz", GB, lambda i: G * i - 2, lambda i: LAND + GB * (i - 1), "hrecv", "hloc")
     arrives("hrecv", 8 * q, [("hq", LAND, LAND + 3 * GB), ("hz", LAND, LAND + 3 * GB)])
 
-    mm("pv", "vq", "vz", 0, "hq", "hz", OWN, GT)
+    mm("pv", "vq", "vz", 0, "hq", "hz", 0, GT)
     cp(("hv", 2, GB), ("pv", 0, G), "a")
     cp(("hv", 0, 2), ("pv", GT - 2, GT), "a")
     left[0]()

@@ -1,29 +1,31 @@
 from concourse.bass import DstId, RemoteDMATransfer
-from concourse.mybir import dt, AluOpType, AxisListType, ActivationFunctionType
+from concourse.mybir import dt, AluOpType, ActivationFunctionType
 
 ALU = AluOpType
 ACT = ActivationFunctionType
 N = 4
-G = 36
+G = 32
 GT = 4 * G
 GB = G + 2
 LAND = GT
 X0 = 16
 X1 = X0 + 512
+XB = 16
 BIG = 1e25
-DUMP = 192
-ROUND4 = 50331648.0
+DUMP = 130
+FW = 776
+CC = 272
 
 SCRATCH = {}
 for _dtype, _names in {
-    "bfloat16": "pb 64 pt 576 xb 2048 ab 2048 wb 512 vb 512 nn 256 cc 256 la 32 lr 32 zb 32 ex 96 rw 96 msg 8 msgin 8 bn 16 bc 16 "
-                "xg 592 sx 576 hb 576 t1 16 t2 16 in2 32 ut 32",
-    "float32": "sc 256 rs 136 xm 264 eq 32 one 32 cnt 32 ncx 32 pr 32 pm 32 col 16 bs 32 bx 24 be 32 br 32 pf 8 pg 8 row 16 mk 32 kd 32 mu 128 "
-               "mb 128 rt 36 cf 36 cfe 36 jv 512 u 32 nk 32 of 32 fw 704 fm 128 gf 32 cm 32 gx 32 bf 32 ix 32 hv 152 wx 512 yb 512 lb0 32 lb1 32",
-    "int32": "pi 8 wi 32 zi 32 bi 32 ki 32",
-    "uint16": "of16 32 ls16 32 sh16 36 ix16 32",
-    "float8_e4m3fn_x4": "pq 144 xq 544 aq 512 wq 128 vq 128 cq 272 hq 272",
-    "uint8": "pz 144 xz 544 az 512 wz 128 vz 128 cz 272 hz 272",
+    "bfloat16": "pb 64 pt 576 xb 2064 ab 2048 wb 512 vb 512 nn 256 cc 272 la 64 lr 64 msg 16 msgin 8 bn 16 bc 16 sx 512 hb 512",
+    "float32": "zb 136 sc 256 rs 136 xm 264 eq 64 one 64 cn 64 nk 32 xa 32 rw 32 sf 16 sm 16 bs 32 bx 24 cf 32 ct 32 be 64 br 64 pf 16 pg 16 l4 8 "
+               "row 32 tq 32 mb 32 kn 8 kn2 8 kc 4 kd 32 ji 128 jv 512 fw 776 fm 128 yj 16 col 8 u 32 t1 16 t2 16 in2 32 ut 32 gf 32 cm 32 gx 32 "
+               "bf 32 ix 32 hv 136 wx 512 yb 512 lb0 32 lb1 32",
+    "int32": "pi 12 vi 2 ci 2 wi 32 zi 32 bi 32 ki 32",
+    "uint16": "lg16 4 of16 32 off16 2 ls16 32 ix16 32",
+    "float8_e4m3fn_x4": "pq 144 xq 544 bq 144 aq 512 wq 128 vq 128 cq 224 hq 232",
+    "uint8": "pz 144 xz 544 bz 144 az 512 wz 128 vz 128 cz 224 hz 232",
 }.items():
     _l = _names.split()
     for _n, _w in zip(_l[::2], _l[1::2]):
@@ -131,6 +133,9 @@ def rank_program(g, core, T, topo):
         b = ap(bias) if isinstance(bias, tuple) else bias
         emit("a", lambda: g.scalar.activation(ap(o), ap(x), ACT.Identity, bias=b, scale=scale), r, [span(o)])
 
+    def total(o, x, n):
+        emit("a", lambda: g.scalar.activation(A("yj", 0, n), ap(x), ACT.Copy, accum_out=ap(o)), [span(x)], [("yj", 0, n), span(o)])
+
     def fill(o, c):
         emit("v", lambda: g.vector.memset(ap(o), c), [], [span(o)])
 
@@ -138,13 +143,9 @@ def rank_program(g, core, T, topo):
         emit("v", lambda: g.vector.transpose(ap(o), ap(x)), [span(x)], [span(o)])
 
     def scan(o, d0, d1, init, op0, op1):
-        emit("v", lambda: g.vector.tensor_tensor_scan(ap(o), ap(d0), ap(d1), init, op0, op1), [span(d0), span(d1)], [span(o)])
-
-    def red(o, x, op):
-        emit("v", lambda: g.vector.tensor_reduce(ap(o), ap(x), AxisListType.X, op), [span(x)], [span(o)])
-
-    def spread(o, x):
-        act(o, ("zb", 0, 32), x)
+        r = [span(d0), span(d1)] + ([span(init)] if isinstance(init, tuple) else [])
+        c = ap(init) if isinstance(init, tuple) else init
+        emit("v", lambda: g.vector.tensor_tensor_scan(ap(o), ap(d0), ap(d1), c, op0, op1), r, [span(o)])
 
     def quant(cq, cz, a, src, b, n):
         emit("v", lambda: g.vector.quantize_mx(A(cq, a, a + n), A(cz, a, a + n), A(src, 4 * b, 4 * b + 4 * n)),
@@ -160,9 +161,9 @@ def rank_program(g, core, T, topo):
         else:
             emit("g", lambda: g.iota(ap(o), pattern, base, cm, allow_small_or_imprecise_dtypes=True), [], [span(o)])
 
-    def pick(q, o, win, width, off, a, b):
-        w = T[win][:, 0:width].indirect(T[off][:, a:b])
-        r = [(win, 0, width), (off, a, b)]
+    def pick(q, o, win, off, a, b):
+        w = ap(win).indirect(T[off][:, a:b])
+        r = [span(win), (off, a, b)]
         if q == "v":
             emit("v", lambda: g.vector.tensor_copy(ap(o), w), r, [span(o)])
         else:
@@ -179,63 +180,40 @@ def rank_program(g, core, T, topo):
         return DstId(rid=rid, pnc=pid)
 
     dma("a", "dp", A("pb", 0, 64), T.p[:, 0:64], [], [("pb", 0, 64)])
-    for k, que in ((0, "s"), (3, "a"), (1, "s"), (2, "a")):
-        dma(que, "dx%d" % k, A("xb", 512 * k, 512 * k + 512), T.x[:, 512 * k:512 * k + 512], [], [("xb", 512 * k, 512 * k + 512)])
+    for k, que in enumerate("sasa"):
+        c = XB + 512 * k
+        dma(que, "dx%d" % k, A("xb", c, c + 512), T.x[:, 512 * k:512 * k + 512], [], [("xb", c, c + 512)])
     dma("s", "da", A("ab", 0, 2048), T.a[:, 0:2048], [], [("ab", 0, 2048)])
 
-    iota(("pi", 0, 1), [[0, 1]], 0, 1)
-    iota(("mu", 0, 128), [[0, 32], [1, 4]], 0)
+    iota(("pi", 0, 2), [[-15, 2]], 15, 1)
     iota(("row", 0, 16), [[1, 16]], 0)
-    first = [(3 - (s + 1 + k) % N) for k in range(4)]
-    k = 0
-    while k < 4:
-        n = 1
-        while k + n < 4 and first[k + n] == first[k + n - 1] - 1:
-            n += 1
-        iota(("rt", G // 4 * k, G // 4 * (k + n)), [[-1, n], [-16, G // 4]], 4 * (G - 1) + first[k] + 1)
-        k += n
-    iota(("kd", 0, 32), [[16, 32]], DUMP)
-    iota(("jv", 0, 128), [[4, 8], [128, 16]], 0)
-    fill(("zb", 0, 32), 0.0)
+    iota(("tq", 0, 32), [[0, 8], [1, 4]], 0)
+    iota(("kc", 0, 4), [[32, 4]], 0)
+    iota(("ji", 0, 128), [[4, 8], [128, 16]], 0)
+    iota(("kd", 0, 32), [[-1, 32]], DUMP + 511)
+    iota(("kn", 0, 2), [[2, 2]], s - 6)
+    fill(("zb", 0, 136), 0.0)
     fill(("pt", 0, 576), 0.0)
-    fill(("rs", 0, 136), BIG)
-    fill(("xm", 0, 1), -BIG)
-    fill(("bx", 0, 1), -BIG)
-    fill(("rs", 0, 136, 16), -BIG)
-    cp(("eq", 0, 1), ("zb", 0, 1), "a")
-    cp(("pr", 16, 17), ("zb", 0, 1), "a")
-    act(("one", 0, 32), ("zb", 0, 32), 1.0)
-    cp(("xg", 0, 16), ("zb", 0, 16), "a")
-    cp(("xg", 528, 560), ("zb", 0, 32), "a")
-    cp(("xg", 560, 592), ("zb", 0, 32), "a")
-    ts(("pi", 1, 2), ("pi", 0, 1), 15, None, ALU.bitwise_and)
-    ts(("pi", 2, 3), ("pi", 0, 1), 3, None, ALU.bitwise_and)
-    ts(("pi", 3, 4), ("pi", 0, 1), 2, 3, ALU.logical_shift_right, ALU.bitwise_and)
-    ts(("pi", 4, 5), ("pi", 0, 1), 4, 1, ALU.logical_shift_right, ALU.bitwise_and)
-    cp(("pf", 1, 5), ("pi", 1, 5))
-    p16, p4, pd4, pd16 = [("pf", k, k + 1) for k in (1, 2, 3, 4)]
-    ts(("mb", 0, 128), ("mu", 0, 128), pd4, -BIG, ALU.is_equal, ALU.mult)
-    ts(("mk", 0, 16), ("row", 0, 16), p16, None, ALU.is_equal)
+    cp(("xb", 0, XB), ("zb", 0, XB), "a")
+    act(("rs", 0, 136), ("zb", 0, 136), BIG)
+    for o, c in ((2, 15), (4, 3)):
+        ts(("pi", o, o + 2), ("pi", 0, 2), c, None, ALU.bitwise_and)
+    for o, c, d in ((6, 2, 3), (8, 3, 1), (10, 4, 1)):
+        ts(("pi", o, o + 2), ("pi", 0, 2), c, d, ALU.logical_shift_right, ALU.bitwise_and)
     for k in range(4):
         cp(("pt", 64 + 128 * k, 128 + 128 * k), ("pb", 0, 64), "va"[k // 2])
+    act(("rs", 0, 136, 16), ("zb", 0, 9), -BIG)
+    act(("xm", 0, 1), ("zb", 0, 1), -BIG)
+    act(("bx", 0, 1), ("zb", 0, 1), -BIG)
     quant("pq", "pz", 0, "pt", 0, 144)
-    act(("pg", 0, 1), p4, 0.0, 0.25)
-    act(("pg", 1, 2), pd16, 1.0, -1.0)
-    act(("pg", 2, 3), pd4, ("pg", 0, 1), -4.0)
-    cp(("mk", 16, 32), ("mk", 0, 16), "a")
-    for k in (1, 2, 3):
-        act(("jv", 128 * k, 128 * k + 128), ("jv", 0, 128), 32.0 * k)
-    act(("fw", 0, 128), ("jv", 0, 128), 0.0, 0.0)
-    act(("kd", 0, 32), ("kd", 0, 32), p16)
-    act(("cf", 0, G), ("rt", 0, G), ("pg", 2, 3))
 
-    def border(d, a, za, b, zb, rsem):
+    def border(d, a, za, bq, b, bz, zb, rsem):
         e = shared(core, [d])
         h = len(e) // 2
         moves = [RemoteDMATransfer(dst_ids=[where(d)], dma_engine_mask=mask(e[:h]), remote_sem=T.sem[rsem],
-                                   srcs=[A("xq", a, a + 2).bitcast(dt.uint8)], dsts=[A("xq", b, b + 2).bitcast(dt.uint8)]),
+                                   srcs=[A("xq", a, a + 2).bitcast(dt.uint8)], dsts=[A(bq, b, b + 2).bitcast(dt.uint8)]),
                  RemoteDMATransfer(dst_ids=[where(d)], dma_engine_mask=mask(e[h:]), remote_sem=T.sem[rsem],
-                                   srcs=[A("xz", za, za + 8)], dsts=[A("xz", zb, zb + 8)])]
+                                   srcs=[A("xz", za, za + 8)], dsts=[A(bz, zb, zb + 8)])]
         remote(lambda: g.remote_dma_fused(moves, local_sem=T.sem.bloc), [("xq", a, a + 2), ("xz", za, za + 8)], "bloc", len(e))
 
     def argmax(pl, c, n, bufs):
@@ -245,94 +223,130 @@ def rank_program(g, core, T, topo):
                 lambda: tt((nn_, o, o + w), (sc, o, o + w), (xm, o, o + w), ALU.is_le),
                 lambda: scan((cc, o, o + w), (nn_, o, o + w), (nn_, o, o + w), 0.0, ALU.mult, ALU.add)]
 
+    def quarter(c):
+        n = 2 if c == 0 and s else 0
+        quant("xq", "xz", X0 + 128 * c - n, "xb", XB // 4 + 128 * c - n, 128 + n)
+
+    def score(c):
+        mm("pl%d" % (c // 2), "pq", "pz", 16 - 16 * (c % 2), "xq", "xz", X0 + 128 * c, 128, c % 2 == 0, c % 2 == 1)
+
     edge = ("bs", "bx", "bn", "bc", 0, 16)
-
-    for P, quarters in enumerate(((0, 3), (1, 2))):
-        pl = "pl%d" % P
-        for h, c in enumerate(quarters):
-            quant("xq", "xz", X0 + 128 * c, "xb", 128 * c, 128)
-            if c == 0 and s > 0:
-                border(T.cores[s - 1], X0, X0, X1, X1, "rrecv")
-                arrives("lrecv", len(shared(T.cores[s - 1], [core])), [("xq", X0 - 2, X0), ("xz", X0 - 8, X0)])
-            if c == 3 and s < N - 1:
-                border(T.cores[s + 1], X1 - 2, X1 - 8, X0 - 2, X0 - 8, "lrecv")
-                arrives("rrecv", len(shared(T.cores[s + 1], [core])), [("xq", X1, X1 + 2), ("xz", X1, X1 + 8)])
-            mm(pl, "pq", "pz", 16 - 16 * h, "xq", "xz", X0 + 128 * c, 128, h == 0, h == 1)
-        if P == 1 and s < N - 1:
-            mm("pwx", "pq", "pz", 16, "xq", "xz", X1 + 2 - 128, 128)
-        o = 128 * P
-        for f in argmax(pl, 0, 128, ("sc", "xm", "nn", "cc", o, 128)):
-            f()
-        for h, c in enumerate(quarters):
-            for d in range(2):
-                b = 16 * d + 4 * c
-                cp(("la", b, b + 4), ("cc", o + 16 * h + 15, o + 128, 32), "v" if P == 1 and h == 0 else "a")
-    tr(("lr", 0, 32), ("la", 0, 32))
-
+    half0 = argmax("pl0", 0, 128, ("sc", "xm", "nn", "cc", 0, 128))
+    half1 = argmax("pl1", 0, 128, ("sc", "xm", "nn", "cc", 128, 128))
     right = argmax("pwx", 96, 32, edge) if s < N - 1 else [lambda: None] * 4
-    spread(("ex", 32, 64), ("lr", 0, 1))
-    spread(("ex", 64, 96), ("lr", 31, 32))
-    tt(("eq", 1, 32), ("lr", 1, 32), ("lr", 0, 31), ALU.is_equal)
+
+    quarter(0)
+    if s:
+        border(T.cores[s - 1], X0 - 1, X0 - 1, "xq", X1, "xz", X1, "rrecv")
+    if s < N - 1:
+        arrives("rrecv", len(shared(T.cores[s + 1], [core])), [("xq", X1, X1 + 2), ("xz", X1, X1 + 8)])
+    score(0)
+    cp(("pf", 0, 10), ("pi", 2, 12))
+    p16, p4, pd4, pd8, pd16 = [("pf", k, k + 1) for k in (1, 3, 5, 7, 9)]
+    pg = [("pg", k, k + 1) for k in range(16)]
+    quarter(1)
+    score(1)
+    act(("one", 0, 64), ("zb", 0, 64), 1.0)
+    act(("eq", 32, 64), ("zb", 0, 32), 1.0)
+    act(("cc", 256, CC), ("zb", 0, CC - 256), -1.0)
+    for k in range(2):
+        act(pg[2 + k], ("pf", 2 + k, 3 + k), 15.0, 32.0)
+    for k in range(2):
+        act(pg[4 + k], ("pf", 4 + k, 5 + k), pg[2 + k], 16.0)
+    for k in range(2):
+        act(pg[6 + k], ("pf", 6 + k, 7 + k), pg[4 + k], 96.0)
+    act(pg[0], pd16, 1.0, -1.0)
+    act(pg[1], pd4, 3.0, -1.0)
+    act(("l4", 2, 4), ("zb", 0, 2), pg[7])
+    act(pg[9], p16, 0.0, -32.0)
+    act(pg[10], p16, 31.0, -4.0)
+    act(pg[11], pd8, pg[10], 32.0)
+    act(("kd", 0, 32), ("kd", 0, 32), pg[9])
+    act(("kc", 0, 4), ("kc", 0, 4), p4)
+    act(("kn", 0, 2), ("kn", 0, 2), pd8)
+    for k in range(4):
+        act(("jv", 128 * k, 128 * k + 128), ("ji", 0, 128), ("kc", k, k + 1))
+    act(("fw", 0, 128), ("ji", 0, 128), p4, 0.0)
+    ts(pg[8], p16, 0.0, 1.0, ALU.is_equal, ALU.mult)
+    half0[0]()
+    ts(("sm", 0, 16), ("row", 0, 16), p16, None, ALU.not_equal)
+    half0[1]()
+    quarter(2)
+    score(2)
+    quarter(3)
+    if s < N - 1:
+        border(T.cores[s + 1], X1 - 2, X1 - 8, "bq", 14, "bz", 8, "lrecv")
+    if s:
+        arrives("lrecv", len(shared(T.cores[s - 1], [core])), [("bq", 14, 16), ("bz", 8, 16)])
+    score(3)
+    if s < N - 1:
+        mm("pwx", "pq", "pz", 16, "xq", "xz", X1 + 2 - 128, 128)
+    half0[2]()
+    ts(("l4", 0, 2), ("zb", 0, 2), pg[6], pg[8], ALU.add, ALU.add)
+    half0[3]()
+    half1[0]()
+    ts(("mb", 0, 32), ("tq", 0, 32), pg[1], -BIG, ALU.is_equal, ALU.mult)
+    half1[1]()
+    cp(("lg16", 0, 4), ("l4", 0, 4))
+    half1[2]()
+    half1[3]()
+
+    pick("v", ("la", 0, 64), ("cc", 0, CC), "lg16", 0, 4)
     right[0]()
-    scan(("cnt", 0, 32), ("one", 0, 32), ("eq", 0, 32), 0.0, ALU.add, ALU.subtract)
+    tr(("lr", 0, 64), ("la", 0, 64))
     right[1]()
-    ts(("ex", 0, 32), ("zb", 0, 32), ("cnt", 31, 32), None, ALU.add)
+    tt(("eq", 0, 32), ("lr", 32, 64), ("lr", 31, 63), ALU.is_equal)
     right[2]()
-    tr(("rw", 0, 96), ("ex", 0, 96))
+    scan(("cn", 0, 64), ("eq", 0, 64), ("one", 0, 64), 0.0, ALU.add, ALU.subtract)
     right[3]()
+    tt(("nk", 0, 32), ("eq", 0, 32), ("kd", 0, 32), ALU.mult)
+    tr(("rw", 0, 32), ("cn", 32, 64))
+    if s < N - 1:
+        ts(("cf", 0, 32), ("zb", 0, 32), ("bc", 15, 16), ("lr", 63, 64), ALU.add, ALU.is_equal)
+    tt(("xa", 0, 32), ("nk", 0, 32), ("cn", 0, 32), ALU.add)
+    scan(("sf", 0, 16), ("sm", 0, 16), ("rw", 0, 16), 0.0, ALU.mult, ALU.add)
+    if s < N - 1:
+        tr(("ct", 0, 32), ("cf", 0, 32))
+    own = ("sf", 15, 16)
+    nn = ("col", 2, 3)
+    total(nn, ("rw", 0, 16), 16)
+    ts(("of16", 0, 32), ("xa", 0, 32), own, None, ALU.subtract)
     later = [T.cores[d] for d in range(s + 1, N)]
     if later:
-        spread(("be", 0, 32), ("bc", 15, 16))
-    act(("ncx", 0, 32), ("cnt", 0, 32), ("cnt", 31, 32), -1.0)
-    tt(("pr", 17, 32), ("rw", 33, 48), ("rw", 64, 79), ALU.is_equal)
-    if later:
-        tr(("br", 0, 32), ("be", 0, 32))
-    scan(("pr", 0, 16), ("rw", 0, 16), ("pr", 16, 32), 0.0, ALU.add, ALU.subtract)
-    nn = ("pr", 15, 16)
-    if later:
-        ts(("msg", 0, 1), ("rw", 79, 80), ("br", 30, 31), nn, ALU.is_equal, ALU.subtract)
+        scan(("msg", 0, 16), ("rw", 0, 16), ("zb", 0, 16), ("ct", 31, 32), ALU.add, ALU.add)
         eng = shared(core, later)
         remote(lambda: g.remote_dma_fused([RemoteDMATransfer(dst_ids=[where(d) for d in later], dma_engine_mask=mask(eng), remote_sem=T.sem.mrecv,
-                                                             srcs=[A("msg", 0, 1)], dsts=[A("msgin", s, s + 1) for _ in later])],
-                                          local_sem=T.sem.mloc), [("msg", 0, 1)], "mloc", len(eng))
+                                                             srcs=[A("msg", 15, 16)], dsts=[A("msgin", s, s + 1) for _ in later])],
+                                          local_sem=T.sem.mloc), [("msg", 15, 16)], "mloc", len(eng))
     if s:
         arrives("mrecv", sum(len(shared(T.cores[r], [T.cores[d] for d in range(r + 1, N)])) for r in range(s)), [("msgin", 0, s)])
-    dma("s", "dw", A("wb", 0, 512), T.w[:, 0:512], [("pr", 0, 16)], [("wb", 0, 512)])
+    dma("s", "dw", A("wb", 0, 512), T.w[:, 0:512], [("msg", 15, 16), ("of16", 0, 32)], [("wb", 0, 512)])
     dma("s", "dv", A("vb", 0, 512), T.v[:, 0:512], [], [("vb", 0, 512)])
-    tt(("pm", 0, 32), ("pr", 0, 32), ("mk", 0, 32), ALU.mult)
-    red(("eq", 0, 1), ("pm", 16, 32), ALU.add)
-    red(("col", 2, 3), ("pm", 0, 16), ALU.add)
-    act(("col", 1, 2), nn, -1.0)
-    act(("col", 8, 9), nn, 2.5, -1.0)
-    act(("cfe", 0, G), ("cf", 0, G), ("col", 1, 2))
-    tt(("nk", 0, 32), ("eq", 0, 32), ("kd", 0, 32), ALU.mult)
-    ts(("u", 0, 32), ("ncx", 0, 32), nn, ("col", 2, 3), ALU.add, ALU.subtract)
+    act(("kn2", 0, 2), ("kn", 0, 2), nn)
+    emit("v", lambda: g.vector.tensor_copy(T.fw[:, 0:FW].indirect(T.of16[:, 0:32]), A("jv", 0, 512)),
+         [("jv", 0, 512), ("of16", 0, 32)], [("fw", 0, FW)])
 
-    tt(("of", 0, 32), ("u", 0, 32), ("nk", 0, 32), ALU.max)
-    cp(("of16", 0, 32), ("of", 0, 32))
-    emit("v", lambda: g.vector.tensor_copy(T.fw[:, 0:DUMP + 512].indirect(T.of16[:, 0:32]), A("jv", 0, 512)),
-         [("jv", 0, 512), ("of16", 0, 32)], [("fw", 0, DUMP + 512)])
-    scan(("fm", 0, 128), ("mb", 0, 128), ("fw", 0, 128), 0.0, ALU.add, ALU.max)
-    ts(("ls16", 0, 32), ("fm", 3, 128, 4), p4, None, ALU.add)
-    pick("a", ("xg", 304, 528), "xb", 2048, "ls16", 18, 32)
-    pick("v", ("xg", 16, 304), "xb", 2048, "ls16", 0, 18)
+    Y = ("msgin", 0, 1)
+    if s > 1:
+        Y = ("col", 0, 1)
+        total(Y, ("msgin", 0, s), s)
 
-    E, z, ne3 = ("col", 5, 6), ("col", 10, 11), ("col", 9, 10)
-    Y = 0.0
-    if s == 0:
-        E = ("col", 1, 2)
-        ts(("col", 4, 5), ("col", 8, 9), ROUND4, None, ALU.add)
+    def wrap(k):
+        scan(("fm", 32 * k, 32 * k + 32), ("mb", 0, 32), ("fw", k, 128, 4), 0.0, ALU.add, ALU.max)
+
+    if s:
+        ts(("vi", 0, 2), ("kn2", 0, 2), Y, -1.0, ALU.add, ALU.mult)
     else:
-        Y = ("msgin", 0, 1) if s == 1 else ("col", 3, 4)
-        if s == 2:
-            ts(Y, ("msgin", 0, 1), ("msgin", 1, 2), None, ALU.add)
-        if s == 3:
-            ts(Y, ("msgin", 0, 1), ("msgin", 1, 2), ("msgin", 2, 3), ALU.add, ALU.add)
-        ts(("col", 4, 5), Y, ("col", 8, 9), ROUND4, ALU.add, ALU.add)
-    ts(z, ("col", 4, 5), ROUND4, Y, ALU.subtract, ALU.subtract)
-    ts(("sh16", 0, G), ("cfe", 0, G), z, 4.0, ALU.add, ALU.mult)
-    pick("a", ("sx", 320, 4 * GT), "xg", 592, "sh16", 20, G)
-    pick("v", ("sx", 0, 320), "xg", 592, "sh16", 0, 20)
+        ts(("vi", 0, 2), ("kn2", 0, 2), -1.0, None, ALU.mult)
+    wrap(0)
+    wrap(1)
+    ts(("ci", 0, 2), ("vi", 0, 2), 3, None, ALU.bitwise_and)
+    wrap(2)
+    wrap(3)
+    ts(("off16", 0, 2), ("ci", 0, 2), 32.0, pg[11], ALU.mult, ALU.add)
+    pick("v", ("ls16", 0, 32), ("fm", 0, 128), "off16", 0, 2)
+    pick("a", ("sx", 288, 4 * GT), ("xb", XB, XB + 2048), "ls16", 18, 32)
+    pick("v", ("sx", 0, 288), ("xb", XB, XB + 2048), "ls16", 0, 18)
     quant("cq", "cz", 0, "sx", 0, GT)
 
     peers = [T.cores[(s + i) % N] for i in (1, 2, 3)]
@@ -358,27 +372,40 @@ def rank_program(g, core, T, topo):
     hop("cq", "cz", G, lambda i: G * (i - 1), lambda i: LAND + G * (3 - i), "crecv", "cloc")
     arrives("crecv", 8 * q, [("cq", LAND, LAND + 3 * G), ("cz", LAND, LAND + 3 * G)])
 
-    quant("aq", "az", 0, "ab", 0, 512)
-    quant("wq", "wz", 0, "wb", 0, 128)
-    mm("pwx", "wq", "wz", 0, "xq", "xz", X0, 512)
-    cp(("wx", 0, 512), ("pwx", 0, 512), "a")
-    quant("vq", "vz", 0, "vb", 0, 128)
-    ts(("t1", 0, 16), ("u", 0, 16), ("pg", 1, 2), None, ALU.mult)
-    ts(("t2", 0, 16), ("u", 16, 32), pd16, None, ALU.mult)
-    if s:
-        ts(E, Y, -1.0, ("col", 1, 2), ALU.mult, ALU.add)
-    ts(ne3, z, -1.0, ("col", 1, 2), ALU.mult, ALU.subtract)
-    tt(("in2", 0, 16), ("t1", 0, 16), ("t2", 0, 16), ALU.add)
-    tt(("in2", 16, 32), ("t1", 0, 16), ("t2", 0, 16), ALU.add)
-    ts(("lb1", 0, 32), ("u", 0, 32), -1.0, E, ALU.mult, ALU.add)
-    tr(("ut", 0, 32), ("in2", 0, 32))
-    act(("lb0", 0, 32), ("lr", 0, 32), 15.0, -1.0)
-    dma("s", "dl0", T.lb[0:1, :], T.lb0[0:16, :], [("lb0", 0, 32)], [])
-    dma("s", "dl1", T.lb[1:2, :], T.lb1[0:16, :], [("lb1", 0, 32)], [])
     left = [lambda: None] * 4
     if s:
-        mm("pl1", "pq", "pz", 16, "xq", "xz", X0 - 2, 128)
+        quant("bq", "bz", 16, "xb", XB // 4, 128)
+        mm("pl1", "pq", "pz", 16, "bq", "bz", 14, 128)
         left = argmax("pl1", 0, 32, edge)
+        act(("be", 32, 64), ("zb", 0, 32), ("lr", 32, 33))
+    act(("lb0", 0, 32), ("lr", 32, 64), 15.0, -1.0)
+    quant("aq", "az", 0, "ab", 0, 512)
+    left[0]()
+    quant("wq", "wz", 0, "wb", 0, 128)
+    mm("pwx", "wq", "wz", 0, "xq", "xz", X0, 512)
+    left[1]()
+    quant("vq", "vz", 0, "vb", 0, 128)
+    left[2]()
+    nE = ("col", 1, 2)
+    ts(("u", 0, 32), ("cn", 0, 32), own, None, ALU.subtract)
+    if s:
+        ts(nE, nn, Y, 1.0, ALU.add, ALU.add)
+    else:
+        ts(nE, nn, 1.0, None, ALU.add)
+    left[3]()
+    if s:
+        act(("be", 0, 32), ("zb", 0, 32), ("bc", 15, 16))
+    cp(("wx", 0, 512), ("pwx", 0, 512), "a")
+    ts(("t1", 0, 16), ("u", 0, 16), pg[0], None, ALU.mult)
+    ts(("t2", 0, 16), ("u", 16, 32), pd16, None, ALU.mult)
+    ts(("lb1", 0, 32), ("u", 0, 32), nE, -1.0, ALU.add, ALU.mult)
+    tt(("in2", 0, 16), ("t1", 0, 16), ("t2", 0, 16), ALU.add)
+    tt(("in2", 16, 32), ("t1", 0, 16), ("t2", 0, 16), ALU.add)
+    if s:
+        tr(("br", 0, 64), ("be", 0, 64))
+    tr(("ut", 0, 32), ("in2", 0, 32))
+    dma("s", "dl0", T.lb[0:1, :], T.lb0[0:16, :], [("lb0", 0, 32)], [])
+    dma("s", "dl1", T.lb[1:2, :], T.lb1[0:16, :], [("lb1", 0, 32)], [])
 
     for i in range(4):
         mm("pa%d" % i, "aq", "az", 128 * i, "cq", "cz", 3 * G, GT)
@@ -396,27 +423,22 @@ def rank_program(g, core, T, topo):
     mm("pv", "vq", "vz", 0, "hq", "hz", 0, GT)
     cp(("hv", 2, GB), ("pv", 0, G), "a")
     cp(("hv", 0, 2), ("pv", GT - 2, GT), "a")
-    left[0]()
-    ts(("wi", 0, 32), ("ut", 0, 32), ne3, 3.0, ALU.add, ALU.add)
-    left[1]()
-    ts(("zi", 0, 32), ("ut", 0, 32), ne3, float(s + 4), ALU.add, ALU.add)
-    left[2]()
+    for d in range(2):
+        emit("v", lambda: g.vector.tensor_copy(T.wi[:, d:32:2], A("ut", 16 * d, 16 * d + 16)), [("ut", 0, 32)], [("wi", 16 * d, 16 * d + 16)])
     ts(("ki", 0, 32), ("wi", 0, 32), 2, None, ALU.logical_shift_right)
-    left[3]()
+    ts(("zi", 0, 32), ("wi", 0, 32), nE, float(s + 1024), ALU.add, ALU.add)
     if s:
-        spread(("be", 0, 32), ("bc", 15, 16))
-    ts(("bi", 0, 32), ("zi", 0, 32), 3, None, ALU.bitwise_and)
+        ts(("cm", 0, 32), ("wi", 0, 32), nn, -1.0, ALU.add, ALU.is_equal)
+        ts(("col", 3, 4), ("br", 1, 2), ("br", 32, 33), -1.0, ALU.is_equal, ALU.mult)
     ts(("gf", 0, 32), ("ki", 0, 32), -1.0, float(G), ALU.mult, ALU.add)
+    ts(("bi", 0, 32), ("zi", 0, 32), 3, None, ALU.bitwise_and)
+    if s:
+        ts(("cm", 0, 32), ("cm", 0, 32), ("col", 3, 4), 1.0, ALU.mult, ALU.add)
     ts(("bf", 0, 32), ("bi", 0, 32), float(GB), 1.0, ALU.mult, ALU.add)
     if s:
-        tr(("br", 0, 32), ("be", 0, 32))
-        ts(("col", 6, 7), ("br", 1, 2), ("rw", 32, 33), None, ALU.is_equal)
-        ts(("cm", 0, 32), ("ut", 0, 32), ("col", 1, 2), ("col", 6, 7), ALU.is_equal, ALU.mult)
-        ts(("cm", 0, 32), ("cm", 0, 32), -1.0, 1.0, ALU.mult, ALU.add)
         tt(("gx", 0, 32), ("gf", 0, 32), ("cm", 0, 32), ALU.mult)
     tt(("ix", 0, 32), ("gx" if s else "gf", 0, 32), ("bf", 0, 32), ALU.add)
-    for d in range(2):
-        cp(("ix16", d, 32, 2), ("ix", 16 * d, 16 * d + 16))
+    cp(("ix16", 0, 32), ("ix", 0, 32))
 
     mm("pl0", "vq", "vz", 0, "hq", "hz", LAND + 3 * GB - 128, 128)
     cp(("hv", GB, 4 * GB), ("pl0", 128 - 3 * GB, 128))

from concourse.bass import DstId, RemoteDMATransfer
from concourse.mybir import dt, AluOpType, ActivationFunctionType

ALU = AluOpType
ACT = ActivationFunctionType
N = 4
G = 32
GT = 4 * G
GB = G + 2
LAND = GT
X0 = 16
X1 = X0 + 512
XB = 16
BIG = 1e25
DUMP = 130
FW = 776
CC = 272

SCRATCH = {}
for _dtype, _names in {
    "bfloat16": "pb 64 pt 576 xb 2064 ab 2048 wb 512 vb 512 nn 256 cc 272 la 64 lr 64 msg 16 msgin 8 bn 16 bc 16 sx 512 hb 512",
    "float32": "zb 136 sc 256 rs 136 xm 264 eq 64 one 64 cn 64 nk 32 xa 32 rw 32 sf 16 sm 16 bs 32 bx 24 cf 32 ct 32 be 64 br 64 pf 16 pg 16 l4 8 "
               "row 32 tq 32 mb 32 kn 8 kn2 8 kc 4 kd 32 ji 128 jv 512 fw 776 fm 128 yj 16 col 8 u 32 t1 16 t2 16 in2 32 ut 32 gf 32 cm 32 gx 32 "
               "bf 32 ix 32 hv 136 wx 512 yb 512 lb0 32 lb1 32",
    "int32": "pi 12 vi 2 ci 2 wi 32 zi 32 bi 32 ki 32",
    "uint16": "lg16 4 of16 32 off16 2 ls16 32 ix16 32",
    "float8_e4m3fn_x4": "pq 144 xq 544 bq 144 aq 512 wq 128 vq 128 cq 224 hq 232",
    "uint8": "pz 144 xz 544 bz 144 az 512 wz 128 vz 128 cz 224 hz 232",
}.items():
    _l = _names.split()
    for _n, _w in zip(_l[::2], _l[1::2]):
        SCRATCH[_n] = ("sbuf", [128, int(_w)], _dtype)
for _n in ("pl0", "pl1", "pwx", "pa0", "pa1", "pa2", "pa3", "pv"):
    SCRATCH[_n] = ("psum", [128, 512], "float32")
SEMAPHORES = ["sv", "sa", "st", "sg", "lrecv", "rrecv", "bloc", "mrecv", "mloc", "crecv", "cloc", "hrecv", "hloc",
              "dp", "dx0", "dx1", "dx2", "dx3", "da", "dw", "dv", "dl0", "dl1", "dy0", "dy1", "dy2"]


def tracker(g, T):
    queues = {"v": g.vector, "a": g.scalar, "t": g.tensor, "g": g, "s": g.sync}
    know = {q: {} for q in queues}
    count = {}
    acc = {}
    order = [0]

    def wait(q, tok):
        sem, n, snap = tok
        if know[q].get(sem, 0) < n:
            queues[q].wait_ge(T.sem[sem], n)
            for k, v in snap.items():
                if know[q].get(k, 0) < v:
                    know[q][k] = v
            know[q][sem] = max(n, know[q].get(sem, 0))

    def settle(q, reads, writes):
        deps = []
        for buf, a, b in reads:
            deps += [(o, tok) for (c, d, w, tok, o) in acc.get(buf, []) if w and a < d and c < b]
        for buf, a, b in writes:
            deps += [(o, tok) for (c, d, w, tok, o) in acc.get(buf, []) if a < d and c < b]
        for o, tok in sorted(deps, key=lambda z: -z[0]):
            wait(q, tok)

    def note(tok, reads, writes):
        order[0] += 1
        for buf, a, b in reads:
            acc.setdefault(buf, []).append((a, b, False, tok, order[0]))
        for buf, a, b in writes:
            acc.setdefault(buf, []).append((a, b, True, tok, order[0]))

    def emit(q, call, reads, writes, sem=None, inc=1, chain=False):
        settle(q, reads, [] if chain else writes)
        sem = sem or "s" + q
        call().then_inc(T.sem[sem], inc)
        count[sem] = count.get(sem, 0) + inc
        note((sem, count[sem], dict(know[q])), reads, writes)

    def remote(call, reads, sem, n):
        settle("g", reads, [])
        call()
        count[sem] = count.get(sem, 0) + n

    def arrives(sem, n, writes):
        count[sem] = count.get(sem, 0) + n
        note((sem, n, {}), [], writes)

    def finish():
        for sem, n in count.items():
            wait("g", (sem, n, {}))

    return emit, remote, arrives, finish


def rank_program(g, core, T, topo):
    s = T.rank_of(core)
    if s is None:
        return
    emit, remote, arrives, finish = tracker(g, T)

    def A(name, a, b):
        return T[name][:, a:b]

    def ap(t):
        return T[t[0]][:, t[1]:t[2]:t[3]] if len(t) > 3 else T[t[0]][:, t[1]:t[2]]

    def span(t):
        return (t[0], t[1], t[2])

    def dma(q, sem, out, in_, reads, writes):
        eng = g.sync if q == "s" else g.scalar
        emit(q, lambda: eng.dma_start(out, in_), reads, writes, sem=sem, inc=16)

    def tt(o, x, y, op):
        emit("v", lambda: g.vector.tensor_tensor(ap(o), ap(x), ap(y), op), [span(x), span(y)], [span(o)])

    def ts(o, x, s1, s2, op0, op1=None):
        r = [span(x)] + [span(z) for z in (s1, s2) if isinstance(z, tuple)]
        c1 = ap(s1) if isinstance(s1, tuple) else s1
        c2 = ap(s2) if isinstance(s2, tuple) else s2
        if op1 is None:
            emit("v", lambda: g.vector.tensor_scalar(ap(o), ap(x), c1, None, op0), r, [span(o)])
        else:
            emit("v", lambda: g.vector.tensor_scalar(ap(o), ap(x), c1, c2, op0, op1), r, [span(o)])

    def cp(o, x, q="v"):
        if q == "v":
            emit("v", lambda: g.vector.tensor_copy(ap(o), ap(x)), [span(x)], [span(o)])
        else:
            emit("a", lambda: g.scalar.activation(ap(o), ap(x), ACT.Copy), [span(x)], [span(o)])

    def act(o, x, bias, scale=1.0):
        r = [span(x)] + ([span(bias)] if isinstance(bias, tuple) else [])
        b = ap(bias) if isinstance(bias, tuple) else bias
        emit("a", lambda: g.scalar.activation(ap(o), ap(x), ACT.Identity, bias=b, scale=scale), r, [span(o)])

    def total(o, x, n):
        emit("a", lambda: g.scalar.activation(A("yj", 0, n), ap(x), ACT.Copy, accum_out=ap(o)), [span(x)], [("yj", 0, n), span(o)])

    def fill(o, c):
        emit("v", lambda: g.vector.memset(ap(o), c), [], [span(o)])

    def tr(o, x):
        emit("v", lambda: g.vector.transpose(ap(o), ap(x)), [span(x)], [span(o)])

    def scan(o, d0, d1, init, op0, op1):
        r = [span(d0), span(d1)] + ([span(init)] if isinstance(init, tuple) else [])
        c = ap(init) if isinstance(init, tuple) else init
        emit("v", lambda: g.vector.tensor_tensor_scan(ap(o), ap(d0), ap(d1), c, op0, op1), r, [span(o)])

    def quant(cq, cz, a, src, b, n):
        emit("v", lambda: g.vector.quantize_mx(A(cq, a, a + n), A(cz, a, a + n), A(src, 4 * b, 4 * b + 4 * n)),
             [(src, 4 * b, 4 * b + 4 * n)], [(cq, a, a + n), (cz, a, a + n)])

    def mm(o, lq, lz, a, rq, rz, b, n, start=True, stop=True):
        emit("t", lambda: g.tensor.matmul_mx(A(o, 0, n), A(lq, a, a + 128), A(lz, a, a + 128), A(rq, b, b + n), A(rz, b, b + n), start, stop),
             [(lq, a, a + 128), (lz, a, a + 128), (rq, b, b + n), (rz, b, b + n)], [(o, 0, 512)], chain=not start)

    def iota(o, pattern, base, cm=0):
        if o[0] == "pi":
            emit("g", lambda: g.iota(ap(o), pattern, base, cm), [], [span(o)])
        else:
            emit("g", lambda: g.iota(ap(o), pattern, base, cm, allow_small_or_imprecise_dtypes=True), [], [span(o)])

    def pick(q, o, win, off, a, b):
        w = ap(win).indirect(T[off][:, a:b])
        r = [span(win), (off, a, b)]
        if q == "v":
            emit("v", lambda: g.vector.tensor_copy(ap(o), w), r, [span(o)])
        else:
            emit("a", lambda: g.scalar.activation(ap(o), w, ACT.Copy), r, [span(o)])

    def shared(src, dsts):
        return [e for e in topo.engines(src, dsts[0]) if all(e in topo.engines(src, d) for d in dsts)]

    def mask(engines):
        return sum(1 << e for e in engines)

    def where(d):
        rid, pid, _ = topo.addr(d)
        return DstId(rid=rid, pnc=pid)

    dma("a", "dp", A("pb", 0, 64), T.p[:, 0:64], [], [("pb", 0, 64)])
    for k, que in enumerate("sasa"):
        c = XB + 512 * k
        dma(que, "dx%d" % k, A("xb", c, c + 512), T.x[:, 512 * k:512 * k + 512], [], [("xb", c, c + 512)])
    dma("s", "da", A("ab", 0, 2048), T.a[:, 0:2048], [], [("ab", 0, 2048)])

    iota(("pi", 0, 2), [[-15, 2]], 15, 1)
    iota(("row", 0, 16), [[1, 16]], 0)
    iota(("tq", 0, 32), [[0, 8], [1, 4]], 0)
    iota(("kc", 0, 4), [[32, 4]], 0)
    iota(("ji", 0, 128), [[4, 8], [128, 16]], 0)
    iota(("kd", 0, 32), [[-1, 32]], DUMP + 511)
    iota(("kn", 0, 2), [[2, 2]], s - 6)
    fill(("zb", 0, 136), 0.0)
    fill(("pt", 0, 576), 0.0)
    cp(("xb", 0, XB), ("zb", 0, XB), "a")
    act(("rs", 0, 136), ("zb", 0, 136), BIG)
    for o, c in ((2, 15), (4, 3)):
        ts(("pi", o, o + 2), ("pi", 0, 2), c, None, ALU.bitwise_and)
    for o, c, d in ((6, 2, 3), (8, 3, 1), (10, 4, 1)):
        ts(("pi", o, o + 2), ("pi", 0, 2), c, d, ALU.logical_shift_right, ALU.bitwise_and)
    for k in range(4):
        cp(("pt", 64 + 128 * k, 128 + 128 * k), ("pb", 0, 64), "va"[k // 2])
    act(("rs", 0, 136, 16), ("zb", 0, 9), -BIG)
    act(("xm", 0, 1), ("zb", 0, 1), -BIG)
    act(("bx", 0, 1), ("zb", 0, 1), -BIG)
    quant("pq", "pz", 0, "pt", 0, 144)

    def border(d, a, za, bq, b, bz, zb, rsem):
        e = shared(core, [d])
        h = len(e) // 2
        moves = [RemoteDMATransfer(dst_ids=[where(d)], dma_engine_mask=mask(e[:h]), remote_sem=T.sem[rsem],
                                   srcs=[A("xq", a, a + 2).bitcast(dt.uint8)], dsts=[A(bq, b, b + 2).bitcast(dt.uint8)]),
                 RemoteDMATransfer(dst_ids=[where(d)], dma_engine_mask=mask(e[h:]), remote_sem=T.sem[rsem],
                                   srcs=[A("xz", za, za + 8)], dsts=[A(bz, zb, zb + 8)])]
        remote(lambda: g.remote_dma_fused(moves, local_sem=T.sem.bloc), [("xq", a, a + 2), ("xz", za, za + 8)], "bloc", len(e))

    def argmax(pl, c, n, bufs):
        sc, xm, nn_, cc, o, w = bufs
        return [lambda: tr((sc, o, o + n), (pl, c, c + n)),
                lambda: scan((xm, o + 1, o + w + 1), (sc, o, o + w), ("rs", 1, w + 1), -BIG, ALU.max, ALU.min),
                lambda: tt((nn_, o, o + w), (sc, o, o + w), (xm, o, o + w), ALU.is_le),
                lambda: scan((cc, o, o + w), (nn_, o, o + w), (nn_, o, o + w), 0.0, ALU.mult, ALU.add)]

    def quarter(c):
        n = 2 if c == 0 and s else 0
        quant("xq", "xz", X0 + 128 * c - n, "xb", XB // 4 + 128 * c - n, 128 + n)

    def score(c):
        mm("pl%d" % (c // 2), "pq", "pz", 16 - 16 * (c % 2), "xq", "xz", X0 + 128 * c, 128, c % 2 == 0, c % 2 == 1)

    edge = ("bs", "bx", "bn", "bc", 0, 16)
    half0 = argmax("pl0", 0, 128, ("sc", "xm", "nn", "cc", 0, 128))
    half1 = argmax("pl1", 0, 128, ("sc", "xm", "nn", "cc", 128, 128))
    right = argmax("pwx", 96, 32, edge) if s < N - 1 else [lambda: None] * 4

    quarter(0)
    if s:
        border(T.cores[s - 1], X0 - 1, X0 - 1, "xq", X1, "xz", X1, "rrecv")
    if s < N - 1:
        arrives("rrecv", len(shared(T.cores[s + 1], [core])), [("xq", X1, X1 + 2), ("xz", X1, X1 + 8)])
    score(0)
    cp(("pf", 0, 10), ("pi", 2, 12))
    p16, p4, pd4, pd8, pd16 = [("pf", k, k + 1) for k in (1, 3, 5, 7, 9)]
    pg = [("pg", k, k + 1) for k in range(16)]
    quarter(1)
    score(1)
    act(("one", 0, 64), ("zb", 0, 64), 1.0)
    act(("eq", 32, 64), ("zb", 0, 32), 1.0)
    act(("cc", 256, CC), ("zb", 0, CC - 256), -1.0)
    for k in range(2):
        act(pg[2 + k], ("pf", 2 + k, 3 + k), 15.0, 32.0)
    for k in range(2):
        act(pg[4 + k], ("pf", 4 + k, 5 + k), pg[2 + k], 16.0)
    for k in range(2):
        act(pg[6 + k], ("pf", 6 + k, 7 + k), pg[4 + k], 96.0)
    act(pg[0], pd16, 1.0, -1.0)
    act(pg[1], pd4, 3.0, -1.0)
    act(("l4", 2, 4), ("zb", 0, 2), pg[7])
    act(pg[9], p16, 0.0, -32.0)
    act(pg[10], p16, 31.0, -4.0)
    act(pg[11], pd8, pg[10], 32.0)
    act(("kd", 0, 32), ("kd", 0, 32), pg[9])
    act(("kc", 0, 4), ("kc", 0, 4), p4)
    act(("kn", 0, 2), ("kn", 0, 2), pd8)
    for k in range(4):
        act(("jv", 128 * k, 128 * k + 128), ("ji", 0, 128), ("kc", k, k + 1))
    act(("fw", 0, 128), ("ji", 0, 128), p4, 0.0)
    ts(pg[8], p16, 0.0, 1.0, ALU.is_equal, ALU.mult)
    half0[0]()
    ts(("sm", 0, 16), ("row", 0, 16), p16, None, ALU.not_equal)
    half0[1]()
    quarter(2)
    score(2)
    quarter(3)
    if s < N - 1:
        border(T.cores[s + 1], X1 - 2, X1 - 8, "bq", 14, "bz", 8, "lrecv")
    if s:
        arrives("lrecv", len(shared(T.cores[s - 1], [core])), [("bq", 14, 16), ("bz", 8, 16)])
    score(3)
    if s < N - 1:
        mm("pwx", "pq", "pz", 16, "xq", "xz", X1 + 2 - 128, 128)
    half0[2]()
    ts(("l4", 0, 2), ("zb", 0, 2), pg[6], pg[8], ALU.add, ALU.add)
    half0[3]()
    half1[0]()
    ts(("mb", 0, 32), ("tq", 0, 32), pg[1], -BIG, ALU.is_equal, ALU.mult)
    half1[1]()
    cp(("lg16", 0, 4), ("l4", 0, 4))
    half1[2]()
    half1[3]()

    pick("v", ("la", 0, 64), ("cc", 0, CC), "lg16", 0, 4)
    right[0]()
    tr(("lr", 0, 64), ("la", 0, 64))
    right[1]()
    tt(("eq", 0, 32), ("lr", 32, 64), ("lr", 31, 63), ALU.is_equal)
    right[2]()
    scan(("cn", 0, 64), ("eq", 0, 64), ("one", 0, 64), 0.0, ALU.add, ALU.subtract)
    right[3]()
    tt(("nk", 0, 32), ("eq", 0, 32), ("kd", 0, 32), ALU.mult)
    tr(("rw", 0, 32), ("cn", 32, 64))
    if s < N - 1:
        ts(("cf", 0, 32), ("zb", 0, 32), ("bc", 15, 16), ("lr", 63, 64), ALU.add, ALU.is_equal)
    tt(("xa", 0, 32), ("nk", 0, 32), ("cn", 0, 32), ALU.add)
    scan(("sf", 0, 16), ("sm", 0, 16), ("rw", 0, 16), 0.0, ALU.mult, ALU.add)
    if s < N - 1:
        tr(("ct", 0, 32), ("cf", 0, 32))
    own = ("sf", 15, 16)
    nn = ("col", 2, 3)
    total(nn, ("rw", 0, 16), 16)
    ts(("of16", 0, 32), ("xa", 0, 32), own, None, ALU.subtract)
    later = [T.cores[d] for d in range(s + 1, N)]
    if later:
        scan(("msg", 0, 16), ("rw", 0, 16), ("zb", 0, 16), ("ct", 31, 32), ALU.add, ALU.add)
        eng = shared(core, later)
        remote(lambda: g.remote_dma_fused([RemoteDMATransfer(dst_ids=[where(d) for d in later], dma_engine_mask=mask(eng), remote_sem=T.sem.mrecv,
                                                             srcs=[A("msg", 15, 16)], dsts=[A("msgin", s, s + 1) for _ in later])],
                                          local_sem=T.sem.mloc), [("msg", 15, 16)], "mloc", len(eng))
    if s:
        arrives("mrecv", sum(len(shared(T.cores[r], [T.cores[d] for d in range(r + 1, N)])) for r in range(s)), [("msgin", 0, s)])
    dma("s", "dw", A("wb", 0, 512), T.w[:, 0:512], [("msg", 15, 16), ("of16", 0, 32)], [("wb", 0, 512)])
    dma("s", "dv", A("vb", 0, 512), T.v[:, 0:512], [], [("vb", 0, 512)])
    act(("kn2", 0, 2), ("kn", 0, 2), nn)
    emit("v", lambda: g.vector.tensor_copy(T.fw[:, 0:FW].indirect(T.of16[:, 0:32]), A("jv", 0, 512)),
         [("jv", 0, 512), ("of16", 0, 32)], [("fw", 0, FW)])

    Y = ("msgin", 0, 1)
    if s > 1:
        Y = ("col", 0, 1)
        total(Y, ("msgin", 0, s), s)

    def wrap(k):
        scan(("fm", 32 * k, 32 * k + 32), ("mb", 0, 32), ("fw", k, 128, 4), 0.0, ALU.add, ALU.max)

    if s:
        ts(("vi", 0, 2), ("kn2", 0, 2), Y, -1.0, ALU.add, ALU.mult)
    else:
        ts(("vi", 0, 2), ("kn2", 0, 2), -1.0, None, ALU.mult)
    wrap(0)
    wrap(1)
    ts(("ci", 0, 2), ("vi", 0, 2), 3, None, ALU.bitwise_and)
    wrap(2)
    wrap(3)
    ts(("off16", 0, 2), ("ci", 0, 2), 32.0, pg[11], ALU.mult, ALU.add)
    pick("v", ("ls16", 0, 32), ("fm", 0, 128), "off16", 0, 2)
    pick("a", ("sx", 288, 4 * GT), ("xb", XB, XB + 2048), "ls16", 18, 32)
    pick("v", ("sx", 0, 288), ("xb", XB, XB + 2048), "ls16", 0, 18)
    quant("cq", "cz", 0, "sx", 0, GT)

    peers = [T.cores[(s + i) % N] for i in (1, 2, 3)]
    eng = shared(core, peers)
    q = len(eng) // 4
    code_eng = [eng[0:2 * q], eng[2 * q:3 * q], eng[3 * q:4 * q]]
    scale_eng = [eng[0:q], eng[q:2 * q], eng[2 * q:4 * q]]

    def hop(cq, cz, width, src, land, rsem, lsem):
        for codes in (True, False):
            moves = []
            for i in (1, 2, 3):
                a, b = src(i), land(i)
                if codes:
                    x, y = A(cq, a, a + width).bitcast(dt.uint8), A(cq, b, b + width).bitcast(dt.uint8)
                else:
                    x, y = A(cz, a, a + width), A(cz, b, b + width)
                moves.append(RemoteDMATransfer(dst_ids=[where(peers[i - 1])], dma_engine_mask=mask((code_eng if codes else scale_eng)[i - 1]),
                                               remote_sem=T.sem[rsem], srcs=[x], dsts=[y]))
            lo, hi = src(1), src(3) + width
            remote(lambda: g.remote_dma_fused(moves, local_sem=T.sem[lsem]), [(cq, lo, hi), (cz, lo, hi)], lsem, 4 * q)

    hop("cq", "cz", G, lambda i: G * (i - 1), lambda i: LAND + G * (3 - i), "crecv", "cloc")
    arrives("crecv", 8 * q, [("cq", LAND, LAND + 3 * G), ("cz", LAND, LAND + 3 * G)])

    left = [lambda: None] * 4
    if s:
        quant("bq", "bz", 16, "xb", XB // 4, 128)
        mm("pl1", "pq", "pz", 16, "bq", "bz", 14, 128)
        left = argmax("pl1", 0, 32, edge)
        act(("be", 32, 64), ("zb", 0, 32), ("lr", 32, 33))
    act(("lb0", 0, 32), ("lr", 32, 64), 15.0, -1.0)
    quant("aq", "az", 0, "ab", 0, 512)
    left[0]()
    quant("wq", "wz", 0, "wb", 0, 128)
    mm("pwx", "wq", "wz", 0, "xq", "xz", X0, 512)
    left[1]()
    quant("vq", "vz", 0, "vb", 0, 128)
    left[2]()
    nE = ("col", 1, 2)
    ts(("u", 0, 32), ("cn", 0, 32), own, None, ALU.subtract)
    if s:
        ts(nE, nn, Y, 1.0, ALU.add, ALU.add)
    else:
        ts(nE, nn, 1.0, None, ALU.add)
    left[3]()
    if s:
        act(("be", 0, 32), ("zb", 0, 32), ("bc", 15, 16))
    cp(("wx", 0, 512), ("pwx", 0, 512), "a")
    ts(("t1", 0, 16), ("u", 0, 16), pg[0], None, ALU.mult)
    ts(("t2", 0, 16), ("u", 16, 32), pd16, None, ALU.mult)
    ts(("lb1", 0, 32), ("u", 0, 32), nE, -1.0, ALU.add, ALU.mult)
    tt(("in2", 0, 16), ("t1", 0, 16), ("t2", 0, 16), ALU.add)
    tt(("in2", 16, 32), ("t1", 0, 16), ("t2", 0, 16), ALU.add)
    if s:
        tr(("br", 0, 64), ("be", 0, 64))
    tr(("ut", 0, 32), ("in2", 0, 32))
    dma("s", "dl0", T.lb[0:1, :], T.lb0[0:16, :], [("lb0", 0, 32)], [])
    dma("s", "dl1", T.lb[1:2, :], T.lb1[0:16, :], [("lb1", 0, 32)], [])

    for i in range(4):
        mm("pa%d" % i, "aq", "az", 128 * i, "cq", "cz", 3 * G, GT)
    for i in range(4):
        o = ("hb", i, 4 * GT, 4)
        r, w = [("pa%d" % i, 0, 512)], [("hb", i * 4 * GT, i * 4 * GT + 1)]
        if i % 2 == 0:
            emit("a", lambda: g.scalar.activation(ap(o), A("pa%d" % i, 0, GT), ACT.Relu, scale=0.05), r, w)
        else:
            emit("v", lambda: g.vector.tensor_scalar(ap(o), A("pa%d" % i, 0, GT), 0.0, 0.05, ALU.max, ALU.mult), r, w)
    emit("v", lambda: g.vector.quantize_mx(A("hq", 0, GT), A("hz", 0, GT), A("hb", 0, 4 * GT)), [("hb", 0, 16 * GT)], [("hq", 0, GT), ("hz", 0, GT)])
    hop("hq", "hz", GB, lambda i: G * i - 2, lambda i: LAND + GB * (i - 1), "hrecv", "hloc")
    arrives("hrecv", 8 * q, [("hq", LAND, LAND + 3 * GB), ("hz", LAND, LAND + 3 * GB)])

    mm("pv", "vq", "vz", 0, "hq", "hz", 0, GT)
    cp(("hv", 2, GB), ("pv", 0, G), "a")
    cp(("hv", 0, 2), ("pv", GT - 2, GT), "a")
    for d in range(2):
        emit("v", lambda: g.vector.tensor_copy(T.wi[:, d:32:2], A("ut", 16 * d, 16 * d + 16)), [("ut", 0, 32)], [("wi", 16 * d, 16 * d + 16)])
    ts(("ki", 0, 32), ("wi", 0, 32), 2, None, ALU.logical_shift_right)
    ts(("zi", 0, 32), ("wi", 0, 32), nE, float(s + 1024), ALU.add, ALU.add)
    if s:
        ts(("cm", 0, 32), ("wi", 0, 32), nn, -1.0, ALU.add, ALU.is_equal)
        ts(("col", 3, 4), ("br", 1, 2), ("br", 32, 33), -1.0, ALU.is_equal, ALU.mult)
    ts(("gf", 0, 32), ("ki", 0, 32), -1.0, float(G), ALU.mult, ALU.add)
    ts(("bi", 0, 32), ("zi", 0, 32), 3, None, ALU.bitwise_and)
    if s:
        ts(("cm", 0, 32), ("cm", 0, 32), ("col", 3, 4), 1.0, ALU.mult, ALU.add)
    ts(("bf", 0, 32), ("bi", 0, 32), float(GB), 1.0, ALU.mult, ALU.add)
    if s:
        tt(("gx", 0, 32), ("gf", 0, 32), ("cm", 0, 32), ALU.mult)
    tt(("ix", 0, 32), ("gx" if s else "gf", 0, 32), ("bf", 0, 32), ALU.add)
    cp(("ix16", 0, 32), ("ix", 0, 32))

    mm("pl0", "vq", "vz", 0, "hq", "hz", LAND + 3 * GB - 128, 128)
    cp(("hv", GB, 4 * GB), ("pl0", 128 - 3 * GB, 128))
    for k, (c, d) in enumerate(((0, 160), (160, 352), (352, 512))):
        emit("v", lambda: g.vector.tensor_tensor(A("yb", c, d), T.hv[:, 0:4 * GB].indirect(T.ix16[:, c // 16:d // 16]), A("wx", c, d), ALU.add),
             [("hv", 0, 4 * GB), ("ix16", 0, 32), ("wx", c, d)], [("yb", c, d)])
        dma("sas"[k], "dy%d" % k, T.y[:, c:d], A("yb", c, d), [("yb", c, d)], [])
    finish()
